import numpy as np
import ml_dtypes


def mxq(x, axis, fmt="e4m3"):
    dtype, down = {"e4m3": (ml_dtypes.float8_e4m3fn, 7), "e5m2": (ml_dtypes.float8_e5m2, 14)}[fmt]
    v = np.moveaxis(np.asarray(x, np.float32).astype(ml_dtypes.bfloat16).astype(np.float64), axis, -1)
    blocks = v.reshape(v.shape[:-1] + (-1, 32))
    amax = np.abs(blocks).max(-1, keepdims=True)
    byte = np.maximum(np.where(amax > 0, np.frexp(amax)[1] - 1 + 127, 0) - down, 1)
    scale = np.exp2(byte - 127.0)
    codes = (blocks / scale).astype(np.float32).astype(dtype).astype(np.float64)
    return np.moveaxis((codes * scale).reshape(v.shape), -1, axis)


WIDE = False


def mx_kscale(k):
    if not WIDE:
        return np.ones(k)
    levels = np.array([10, -10, 5, -5, 0])
    if k % 512:
        return np.exp2(np.random.permutation(np.resize(levels, k // 32))).repeat(32)
    a = np.empty((k // 512, 16))
    for p in range(k // 512):
        a[p, :8] = np.random.permutation(np.resize(levels, 8))
        for g in range(8):
            far = levels[np.abs(levels - a[p, g]) >= 10]
            a[p, g + 8] = far[np.random.randint(len(far))]
    return np.exp2(a.ravel()).repeat(32)


def f64(x):
    return np.asarray(x).astype(np.float64)


def striped(idx):
    return np.tile(idx.reshape(-1, 16).T, (8, 1)).astype(np.uint16)


def unstriped(offs):
    return offs[:16].T.reshape(-1).astype(np.int64)


E2M1 = np.array([0.0, 0.5, 1.0, 1.5, 2.0, 3.0, 4.0, 6.0, -0.0, -0.5, -1.0, -1.5, -2.0, -3.0, -4.0, -6.0])


def pack_weight(w, fmt):
    k, n = w.shape
    w = f64(np.asarray(w, np.float32).astype(ml_dtypes.bfloat16)).reshape(k // 32, 32, n)
    amax = np.abs(w).max(1)
    if fmt == "e4m3":
        byte = np.frexp(amax)[1] - 1 + 127 - 7
    else:
        mant, ex = np.frexp(amax / 6.0)
        byte = np.where(mant > 0.5, ex, ex - 1) + 127
    byte = np.clip(np.where(amax > 0, byte, 1), 1, 254)
    scaled = (w * np.exp2(127.0 - byte)[:, None, :]).reshape(k, n).astype(np.float32)
    by_word = np.ascontiguousarray(scaled.reshape(k // 512, 128, 4, n).transpose(0, 1, 3, 2))
    if fmt == "e4m3":
        words = by_word.astype(ml_dtypes.float8_e4m3fn).view(np.uint8)
    else:
        c = by_word.astype(ml_dtypes.float4_e2m1fn).view(np.uint8) & 0xF
        words = (c[..., 0::2] | (c[..., 1::2] << 4)).reshape(k // 512, 128, 2 * n)
    return np.ascontiguousarray(words), np.ascontiguousarray(byte.astype(np.uint8).reshape(k // 512, 16, n))


def unpack_weight(words, scales, fmt):
    g, _, n = scales.shape
    words = np.ascontiguousarray(words).reshape(g, 128, n, -1)
    if fmt == "e4m3":
        vals = words.view(ml_dtypes.float8_e4m3fn).astype(np.float64)
    else:
        nib = np.empty((g, 128, n, 4), np.uint8)
        nib[..., 0::2] = words & 0xF
        nib[..., 1::2] = words >> 4
        vals = E2M1[nib]
    vals = vals * np.repeat(np.exp2(scales.astype(np.float64) - 127.0), 8, axis=1)[..., None]
    return vals.transpose(0, 1, 3, 2).reshape(g * 512, n)


def gelu(v):
    return 0.5 * v * (1.0 + np.tanh(np.sqrt(2.0 / np.pi) * (v + 0.044715 * v**3)))


def bf(x):
    return np.asarray(x, np.float32).astype(ml_dtypes.bfloat16)


def planes(Y):
    n, m = Y.shape
    b = f64(bf(Y)).reshape(n // 32, 32, m)
    amax = np.abs(b).max(1)
    byte = np.clip(np.where(amax > 0, np.frexp(amax)[1] - 1 + 127 - 7, 1), 1, 254)
    codes = (b * np.exp2(127.0 - byte)[:, None, :]).reshape(n, m).astype(np.float32).astype(ml_dtypes.float8_e4m3fn).view(np.uint8)
    words = codes.reshape(n // 512, 128, 4, m).transpose(0, 1, 3, 2)
    return np.ascontiguousarray(words), np.ascontiguousarray(byte.astype(np.uint8).reshape(n // 512, 16, m))


K, H, N, T, S, T2, P = 1024, 1024, 512, 4096, 1024, 2048, 1024

def setup_inputs():
    n = np.random.standard_normal
    s = mx_kscale(K)[:, None]
    u = mx_kscale(H)[:, None]
    tab_words, tab_scales = pack_weight(n((K, T)) * s, "e4m3")
    w1 = 1.8 * n((K, H)) / np.sqrt(K) / s
    w2 = 0.7 * n((H, N)) / np.sqrt(H) * np.exp(0.8 * n(N))[None, :] / u
    w2_words, w2_scales = pack_weight(w2, "e2m1")
    return {
        "tab_words": tab_words,
        "tab_scales": tab_scales,
        "offs": striped(np.random.permutation(T)[:S]),
        "offs2": striped(np.random.permutation(T2)[:S]),
        "offs3": striped(np.random.permutation(T2)[:P]),
        "offs4": striped(np.random.permutation(T2)[:P]),
        "w1": w1.astype(np.float32),
        "gain": (np.random.uniform(0.4, 1.0, H) * u[:, 0]).astype(np.float32),
        "wgs": np.exp(0.3 * n((128, S))).astype(np.float32),
        "page0": (n((H, T2)) * u).astype(np.float32),
        "low": (0.6 * n(H)).astype(np.float32),
        "w2_words": w2_words,
        "w2_scales": w2_scales,
    }

def reference(tab_words, tab_scales, offs, offs2, offs3, offs4, w1, gain, wgs, page0, low, w2_words, w2_scales):
    v = unpack_weight(tab_words, tab_scales, "e4m3")[:, unstriped(offs)]
    w2 = unpack_weight(w2_words, w2_scales, "e2m1")
    a = mxq(f64(w1), 0, "e4m3").T @ v
    h = f64(gain)[:, None] * (a + np.tanh(a))
    before = f64(page0)
    page = before.copy()
    page[:, unstriped(offs2)] = np.tile(f64(wgs), (H // 128, 1)) * h
    after = page[:, unstriped(offs3)]
    earlier = before[:, unstriped(offs4)]
    x = np.maximum(after, earlier) + f64(low)[:, None] * np.minimum(after, earlier)
    y = w2.T @ mxq(x, 0, "e4m3")
    words, scales = planes(y)
    return y, words, scales

@@ -1,0 +1,343 @@
+from contextlib import ExitStack
+
+import concourse.mybir as mybir
+from concourse.masks import make_identity
+
+K, H, N, T, S, T2, M = 1024, 1024, 512, 4096, 1024, 2048, 1024
+FLOPS = 2 * K * H * S + 2 * H * N * M
+
+F32 = mybir.dt.float32
+BF16 = mybir.dt.bfloat16
+I32 = mybir.dt.int32
+U32 = mybir.dt.uint32
+U16 = mybir.dt.uint16
+U8 = mybir.dt.uint8
+FP8X4 = mybir.dt.float8_e4m3fn_x4
+FP4X4 = mybir.dt.float4_e2m1fn_x4
+ALU = mybir.AluOpType
+ACT = mybir.ActivationFunctionType
+
+P = 128
+BANK = 512
+SLICES = H // P
+PASSES = 2
+CHUNK = 256
+CHUNKS = M // CHUNK
+
+
+def tile_list_stay_tension_survey_kernel(
+    tc, tab_words, tab_scales, offs, offs2, offs3, offs4, w1, gain, wgs, page0, low, w2_words, w2_scales,
+    out_0, out_1, out_2,
+):
+    nc = tc.nc
+    with ExitStack() as ctx:
+        keep = ctx.enter_context(tc.tile_pool(name="keep", bufs=1))
+        ring = ctx.enter_context(tc.tile_pool(name="ring", bufs=2))
+        psum = ctx.enter_context(tc.psum_pool(name="psum", bufs=2))
+
+        def bank(tag):
+            return psum.tile([P, BANK], F32, name=tag, tag=tag)
+
+        idx_tab = keep.tile([P, S // 16], U16, name="idx_tab")
+        idx_put = keep.tile([P, S // 16], U16, name="idx_put")
+        idx_after = keep.tile([P, M // 16], U16, name="idx_after")
+        idx_before = keep.tile([P, M // 16], U16, name="idx_before")
+
+        tab_sc = keep.tile([P, T], U8, name="tab_sc", align_bytes=64)
+        w2_sc_raw = keep.tile([P, PASSES, N], U8, name="w2_sc_raw")
+        rows = keep.tile([P, P], F32, name="rows")
+        nc.vector.memset(tab_sc[:].bitcast(I32), 0)
+        nc.vector.memset(w2_sc_raw[:].rearrange("p a n -> p (a n)").bitcast(I32), 0)
+        nc.vector.memset(rows[:], 0.0)
+        ident = keep.tile([P, P], F32, name="ident")
+        make_identity(nc, ident[:])
+
+        pages = {}
+        w1_raw = {}
+
+        def load_page(c):
+            pages[c] = ring.tile([P, T2], F32, name="page", tag="page", bufs=4)
+            nc.sync.dma_start(pages[c][:], page0[c * P:(c + 1) * P, :])
+
+        def load_w1(c):
+            w1_raw[c] = ring.tile([P, PASSES, 4, P], F32, name="w1_raw", tag="w1_raw", bufs=3)
+            view = w1.rearrange("(a p j) r -> a p j r", p=P, j=4)
+            for a in range(PASSES):
+                nc.sync.dma_start(w1_raw[c][:, a], view[a, :, :, c * P:(c + 1) * P])
+
+        nc.sync.dma_start(idx_before[:], offs4)
+        load_page(0)
+        w2_raw = keep.tile([P, PASSES, 2 * N], U8, name="w2_raw")
+        nc.sync.dma_start(w2_raw[:].bitcast(I32), w2_words.rearrange("a p n -> p a n").bitcast(I32))
+        load_w1(0)
+        nc.sync.dma_start(idx_tab[:], offs)
+        tab = []
+        for a in range(PASSES):
+            words = ring.tile([P, T], I32, name="tab", tag="big", align_bytes=64)
+            nc.sync.dma_start(words[:], tab_words[a].rearrange("p t i -> p (t i)").bitcast(I32))
+            tab.append(words)
+        wgs_sb = keep.tile([P, S], F32, name="wgs_sb")
+        nc.sync.dma_start(wgs_sb[:], wgs)
+        nc.sync.dma_start(idx_put[:], offs2)
+        load_page(1)
+        load_w1(1)
+        nc.sync.dma_start(idx_after[:], offs3)
+        load_page(2)
+        load_w1(2)
+
+        for q in range(4):
+            nc.gpsimd.dma_start(tab_sc[32 * q:32 * q + 8, :].bitcast(I32), tab_scales[:, 4 * q:4 * q + 4, :].bitcast(I32))
+        nc.gpsimd.dma_start(rows[0:SLICES, :], gain.rearrange("(c p) -> c p", p=P))
+        nc.gpsimd.dma_start(rows[SLICES:2 * SLICES, :], low.rearrange("(c p) -> c p", p=P))
+        for q in range(4):
+            nc.gpsimd.dma_start(
+                w2_sc_raw[32 * q:32 * q + 4].bitcast(I32),
+                w2_scales[:, 4 * q:4 * q + 4, :].rearrange("a r n -> r a n").bitcast(I32),
+            )
+
+        w2_codes = keep.tile([P, PASSES, 4, 2 * P], U8, name="w2_codes", align_bytes=64)
+        w2_sc = keep.tile([P, PASSES, 4, P], U8, name="w2_sc", align_bytes=64)
+        nc.vector.tensor_copy(
+            w2_codes[:].rearrange("p a t (q b) -> p a t q b", b=2),
+            w2_raw[:].rearrange("p a (q t b) -> p a t q b", t=4, b=2),
+        )
+
+        before = {}
+
+        def gather_before(c):
+            before[c] = ring.tile([P, M], F32, name="before", tag="before", bufs=4)
+            nc.vector.tensor_copy(before[c][:], pages[c][:].indirect(idx_before[:]))
+
+        w1_bf = {}
+        w1_q = {}
+
+        def round_w1(c):
+            w1_bf[c] = ring.tile([P, PASSES, P, 4], BF16, name="w1_bf", tag="w1_bf", align_bytes=64)
+            nc.scalar.copy(
+                w1_bf[c][:].rearrange("p a (g i) j -> p a g j i", i=4),
+                w1_raw[c][:].rearrange("p a j (g i) -> p a g j i", i=4),
+            )
+
+        def quantise_w1(c):
+            codes = ring.tile([P, PASSES * P], U32, name="w1_codes", tag="w1_codes", bufs=3, align_bytes=64)
+            scales = ring.tile([P, PASSES * P], U8, name="w1_scales", tag="w1_scales", bufs=3, align_bytes=64)
+            nc.vector.quantize_mx(codes[:].bitcast(FP8X4), scales[:], w1_bf[c][:].rearrange("p a r j -> p (a r j)"))
+            w1_q[c] = (codes, scales)
+
+        gather_before(0)
+        round_w1(0)
+        quantise_w1(0)
+        v_sc = keep.tile([P, S], U8, name="v_sc", align_bytes=64)
+        nc.vector.tensor_copy(v_sc[:], tab_sc[:].indirect(idx_tab[:]))
+        v_codes = [keep.tile([P, S], U32, name="v_codes%d" % a, align_bytes=64) for a in range(PASSES)]
+        nc.vector.tensor_copy(v_codes[0][:], tab[0][:].bitcast(U32).indirect(idx_tab[:]))
+        cols_ps = bank("wd")
+        nc.tensor.transpose(cols_ps[:, 0:P], rows[:], ident[:])
+        cols = keep.tile([P, 4, SLICES], F32, name="cols")
+        nc.vector.tensor_copy(cols[:, 0:2, :], cols_ps[:, 0:2 * SLICES].rearrange("p (k c) -> p k c", k=2))
+        nc.vector.tensor_scalar(cols[:, 2, :], cols[:, 1, :], 1.0, 1.0, ALU.mult, ALU.add)
+        nc.vector.tensor_scalar(cols[:, 3, :], cols[:, 1, :], -1.0, 1.0, ALU.mult, ALU.add)
+
+        nc.vector.tensor_copy(w2_sc[:], w2_sc_raw[:].rearrange("p a (q t) -> p a t q", t=4))
+        for h in range(2):
+            nc.vector.tensor_copy(
+                v_codes[1][:, h * BANK:(h + 1) * BANK], tab[1][:].bitcast(U32).indirect(idx_tab[:, h * 32:(h + 1) * 32])
+            )
+
+        h_rows = {}
+
+        def make_h(c):
+            codes, scales = w1_q[c]
+            h_rows[c] = ring.tile([P, S], F32, name="h_rows", tag="h_rows", bufs=3)
+            a_t = ring.tile([P, S], F32, name="a_t", tag="a_t")
+            tanh_t = ring.tile([P, S], F32, name="tanh_t", tag="tanh_t")
+            for h in range(2):
+                half = slice(h * BANK, (h + 1) * BANK)
+                acc = bank("a")
+                for b in range(4):
+                    j = slice(h * BANK + b * P, h * BANK + (b + 1) * P)
+                    for a in range(PASSES):
+                        nc.tensor.matmul_mx(
+                            acc[:, b * P:(b + 1) * P],
+                            lhsT=v_codes[a][:, j].bitcast(FP8X4), lhsT_scale=v_sc[4 * a:P, j],
+                            rhs=codes[:, a * P:(a + 1) * P].bitcast(FP8X4), rhs_scale=scales[:, a * P:(a + 1) * P],
+                            start=(a == 0), stop=(a == PASSES - 1),
+                        )
+                nc.scalar.activation(tanh_t[:, half], acc[:], ACT.Tanh)
+                nc.scalar.copy(a_t[:, half], acc[:])
+            for h in range(2):
+                half = slice(h * BANK, (h + 1) * BANK)
+                total = bank("u")
+                for b in range(4):
+                    j = slice(h * BANK + b * P, h * BANK + (b + 1) * P)
+                    for term in (0, 1):
+                        nc.tensor.matmul(
+                            total[:, b * P:(b + 1) * P], lhsT=(tanh_t, a_t)[term][:, j], rhs=ident[:],
+                            start=(term == 0), stop=(term == 1), is_transpose=True,
+                        )
+                nc.scalar.activation(h_rows[c][:, half], total[:], ACT.Copy, scale=cols[:, 0, c:c + 1])
+
+        def put(c, pieces):
+            n = S // pieces
+            for h in range(pieces):
+                nc.vector.tensor_tensor(
+                    pages[c][:].indirect(idx_put[:, h * n // 16:(h + 1) * n // 16]),
+                    h_rows[c][:, h * n:(h + 1) * n], wgs_sb[:, h * n:(h + 1) * n], ALU.mult,
+                )
+
+        diff = {}
+
+        def gather_diff(c, m0, m1):
+            if m0 == 0:
+                diff[c] = ring.tile([P, M], F32, name="diff", tag="diff")
+            nc.vector.tensor_tensor(
+                diff[c][:, m0:m1], pages[c][:].indirect(idx_after[:, m0 // 16:m1 // 16]), before[c][:, m0:m1], ALU.subtract
+            )
+
+        term_e = {}
+        term_d = {}
+        term_r = {}
+
+        def scale_before(c):
+            term_e[c] = ring.tile([P, M], F32, name="term_e", tag="term_e")
+            nc.scalar.activation(term_e[c][:], before[c][:], ACT.Copy, scale=cols[:, 2, c:c + 1])
+
+        def diff_terms(c, m0, m1, on_vector):
+            if m0 == 0:
+                term_d[c] = ring.tile([P, M], F32, name="term_d", tag="term_d")
+                term_r[c] = ring.tile([P, M], F32, name="term_r", tag="term_r")
+            nc.scalar.activation(term_d[c][:, m0:m1], diff[c][:, m0:m1], ACT.Copy, scale=cols[:, 1, c:c + 1])
+            if on_vector:
+                nc.vector.tensor_scalar(term_r[c][:, m0:m1], diff[c][:, m0:m1], 0.0, cols[:, 3, c:c + 1], ALU.max, ALU.mult)
+            else:
+                nc.scalar.activation(term_r[c][:, m0:m1], diff[c][:, m0:m1], ACT.Relu)
+                nc.scalar.activation(term_r[c][:, m0:m1], term_r[c][:, m0:m1], ACT.Copy, scale=cols[:, 3, c:c + 1])
+
+        x_t = {}
+
+        def sum_terms(c, m0, m1):
+            b, cl = divmod(c, 4)
+            if b not in x_t:
+                x_t[b] = ring.tile([P, M // P, 2, P, 2], BF16, name="x_t", tag="big", align_bytes=64)
+            blocks = (m1 - m0) // P
+            total = bank("xs")
+            for l in range(blocks):
+                m = slice(m0 + l * P, m0 + (l + 1) * P)
+                for term in range(3):
+                    nc.tensor.matmul(
+                        total[:, l * P:(l + 1) * P], lhsT=(term_e, term_d, term_r)[term][c][:, m], rhs=ident[:],
+                        start=(term == 0), stop=(term == 2), is_transpose=True,
+                    )
+            nc.scalar.copy(
+                x_t[b][:, m0 // P:m1 // P, :, 32 * cl:32 * (cl + 1), :],
+                total[:, 0:blocks * P].rearrange("m (l q u e) -> m l u q e", u=2, e=2, q=32),
+            )
+
+        x_codes = [keep.tile([P, M], U32, name="x_codes%d" % b, align_bytes=64) for b in range(PASSES)]
+        x_sc = [keep.tile([P, M], U8, name="x_sc%d" % b, align_bytes=64) for b in range(PASSES)]
+        x_bf = {}
+
+        def turn_x(b, g):
+            words = x_t[b][:].rearrange("m l u p e -> m (l u p e)").bitcast(F32)
+            turned = bank("wd")
+            for i in range(4):
+                w0 = (4 * g + i) * P
+                nc.tensor.transpose(turned[:, i * P:(i + 1) * P], words[:, w0:w0 + P], ident[:])
+            x_bf[b, g] = ring.tile([P, CHUNK * 4], BF16, name="x_bf", tag="x_bf", bufs=4, align_bytes=64)
+            nc.scalar.copy(
+                x_bf[b, g][:].bitcast(F32).rearrange("p (l m u) -> p l m u", l=2, u=2),
+                turned[:].rearrange("p (l u m) -> p l m u", l=2, u=2),
+            )
+
+        def quantise_x(b, g):
+            m = slice(g * CHUNK, (g + 1) * CHUNK)
+            nc.vector.quantize_mx(x_codes[b][:, m].bitcast(FP8X4), x_sc[b][:, m], x_bf[b, g][:])
+
+        y_codes = keep.tile([P, M], U32, name="y_codes", align_bytes=64)
+        y_sc = keep.tile([P, M], U8, name="y_sc", align_bytes=64)
+        y_view = out_0.rearrange("(p t) m -> p t m", t=4)
+        y_words = out_1[0].rearrange("p m t -> p (m t)").bitcast(I32)
+        y_sb = {}
+        y_bf = {}
+
+        def make_y(g):
+            m = slice(g * CHUNK, (g + 1) * CHUNK)
+            y_sb[g] = ring.tile([P, 4, CHUNK], F32, name="y_sb", tag="y_sb", bufs=3)
+            for h in range(2):
+                acc = bank(("a", "u")[h])
+                for i in range(2):
+                    for b in range(PASSES):
+                        nc.tensor.matmul_mx(
+                            acc[:, i * CHUNK:(i + 1) * CHUNK],
+                            lhsT=w2_codes[:, b, 2 * h + i, :].bitcast(FP4X4), lhsT_scale=w2_sc[:, b, 2 * h + i, :],
+                            rhs=x_codes[b][:, m].bitcast(FP8X4), rhs_scale=x_sc[b][:, m],
+                            start=(b == 0), stop=(b == PASSES - 1),
+                        )
+                nc.scalar.copy(y_sb[g][:, 2 * h:2 * h + 2, :], acc[:].rearrange("p (i m) -> p i m", i=2))
+            nc.sync.dma_start(y_view[:, :, m], y_sb[g][:])
+
+        def round_y(g):
+            y_bf[g] = ring.tile([P, CHUNK, 4], BF16, name="y_bf", tag="y_bf", align_bytes=64)
+            nc.vector.tensor_copy(
+                y_bf[g][:].rearrange("p (g i) t -> p g t i", i=4), y_sb[g][:].rearrange("p t (g i) -> p g t i", i=4)
+            )
+
+        def quantise_y(g):
+            m = slice(g * CHUNK, (g + 1) * CHUNK)
+            nc.vector.quantize_mx(y_codes[:, m].bitcast(FP8X4), y_sc[:, m], y_bf[g][:].rearrange("p m t -> p (m t)"))
+            nc.sync.dma_start(y_words[:, m], y_codes[:, m].bitcast(I32))
+
+        make_h(0)
+        round_w1(1)
+        quantise_w1(1)
+        gather_before(1)
+        make_h(1)
+        round_w1(2)
+        last = SLICES - 1
+        for c in range(SLICES):
+            if c + 3 < SLICES:
+                load_page(c + 3)
+                load_w1(c + 3)
+            put(c, 2 if c == 0 else 1)
+            if c + 2 < SLICES:
+                quantise_w1(c + 2)
+                gather_before(c + 2)
+            if c == 5:
+                for g in range(CHUNKS):
+                    quantise_x(0, g)
+            if c < last:
+                gather_diff(c, 0, M)
+            if c >= 1:
+                diff_terms(c - 1, 0, M, False)
+                for h in range(2):
+                    sum_terms(c - 1, h * BANK, (h + 1) * BANK)
+            if c == 4:
+                for g in range(CHUNKS):
+                    turn_x(0, g)
+            scale_before(c)
+            if c + 2 < SLICES:
+                make_h(c + 2)
+            if c + 3 < SLICES:
+                round_w1(c + 3)
+
+        for step in range(CHUNKS + 4):
+            if step < CHUNKS:
+                gather_diff(last, step * CHUNK, (step + 1) * CHUNK)
+            g = step - 1
+            if 0 <= g < CHUNKS:
+                diff_terms(last, g * CHUNK, (g + 1) * CHUNK, True)
+                sum_terms(last, g * CHUNK, (g + 1) * CHUNK)
+                turn_x(1, g)
+            g = step - 2
+            if 0 <= g < CHUNKS:
+                quantise_x(1, g)
+                make_y(g)
+            g = step - 3
+            if 0 <= g < CHUNKS:
+                round_y(g)
+            g = step - 4
+            if 0 <= g < CHUNKS:
+                quantise_y(g)
+
+        for q in range(4):
+            nc.sync.dma_start(out_2[0, 4 * q:4 * q + 4, :].bitcast(I32), y_sc[32 * q:32 * q + 4, :].bitcast(I32))

@@ -51,6 +51,8 @@ def tile_list_stay_tension_survey_kernel(
         nc.vector.memset(rows[:], 0.0)
         ident = keep.tile([P, P], F32, name="ident")
         make_identity(nc, ident[:])
+        ident_bf = keep.tile([P, P], BF16, name="ident_bf")
+        make_identity(nc, ident_bf[:])
 
         pages = {}
         w1_raw = {}
@@ -59,41 +61,45 @@ def tile_list_stay_tension_survey_kernel(
             pages[c] = ring.tile([P, T2], F32, name="page", tag="page", bufs=4)
             nc.sync.dma_start(pages[c][:], page0[c * P:(c + 1) * P, :])
 
-        def load_w1(c):
-            w1_raw[c] = ring.tile([P, PASSES, 4, P], F32, name="w1_raw", tag="w1_raw", bufs=3)
+        def load_w1(c0, c1):
+            raw = keep.tile([P, PASSES, 4, (c1 - c0) * P], F32, name="w1_raw%d" % c0)
             view = w1.rearrange("(a p j) r -> a p j r", p=P, j=4)
             for a in range(PASSES):
-                nc.sync.dma_start(w1_raw[c][:, a], view[a, :, :, c * P:(c + 1) * P])
+                nc.sync.dma_start(raw[:, a], view[a, :, :, c0 * P:c1 * P])
+            for c in range(c0, c1):
+                w1_raw[c] = raw[:, :, :, (c - c0) * P:(c - c0 + 1) * P]
 
-        nc.sync.dma_start(idx_before[:], offs4)
-        load_page(0)
+        tab = [ring.tile([P, T], I32, name="tab", tag="big%d" % a, bufs=1, align_bytes=64) for a in range(PASSES)]
+
+        def load_tab(a):
+            nc.sync.dma_start(tab[a][:], tab_words[a].rearrange("p t i -> p (t i)").bitcast(I32))
+
+        for tile, lists in ((idx_tab, offs), (idx_before, offs4), (idx_put, offs2), (idx_after, offs3)):
+            nc.sync.dma_start(tile[:], lists)
+        load_tab(0)
+        load_w1(0, 1)
         w2_raw = keep.tile([P, PASSES, 2 * N], U8, name="w2_raw")
         nc.sync.dma_start(w2_raw[:].bitcast(I32), w2_words.rearrange("a p n -> p a n").bitcast(I32))
-        load_w1(0)
-        nc.sync.dma_start(idx_tab[:], offs)
-        tab = []
-        for a in range(PASSES):
-            words = ring.tile([P, T], I32, name="tab", tag="big", align_bytes=64)
-            nc.sync.dma_start(words[:], tab_words[a].rearrange("p t i -> p (t i)").bitcast(I32))
-            tab.append(words)
+        for q in range(4):
+            nc.sync.dma_start(tab_sc[32 * q:32 * q + 8, :].bitcast(I32), tab_scales[:, 4 * q:4 * q + 4, :].bitcast(I32))
+        load_tab(1)
+        load_page(0)
         wgs_sb = keep.tile([P, S], F32, name="wgs_sb")
         nc.sync.dma_start(wgs_sb[:], wgs)
-        nc.sync.dma_start(idx_put[:], offs2)
+        load_w1(1, 2)
         load_page(1)
-        load_w1(1)
-        nc.sync.dma_start(idx_after[:], offs3)
         load_page(2)
-        load_w1(2)
-
+        load_w1(2, 4)
         for q in range(4):
-            nc.gpsimd.dma_start(tab_sc[32 * q:32 * q + 8, :].bitcast(I32), tab_scales[:, 4 * q:4 * q + 4, :].bitcast(I32))
-        nc.gpsimd.dma_start(rows[0:SLICES, :], gain.rearrange("(c p) -> c p", p=P))
-        nc.gpsimd.dma_start(rows[SLICES:2 * SLICES, :], low.rearrange("(c p) -> c p", p=P))
-        for q in range(4):
-            nc.gpsimd.dma_start(
+            nc.sync.dma_start(
                 w2_sc_raw[32 * q:32 * q + 4].bitcast(I32),
                 w2_scales[:, 4 * q:4 * q + 4, :].rearrange("a r n -> r a n").bitcast(I32),
             )
+        load_page(3)
+        load_w1(4, 8)
+
+        nc.gpsimd.dma_start(rows[0:SLICES, :], gain.rearrange("(c p) -> c p", p=P))
+        nc.gpsimd.dma_start(rows[SLICES:2 * SLICES, :], low.rearrange("(c p) -> c p", p=P))
 
         w2_codes = keep.tile([P, PASSES, 4, 2 * P], U8, name="w2_codes", align_bytes=64)
         w2_sc = keep.tile([P, PASSES, 4, P], U8, name="w2_sc", align_bytes=64)
@@ -105,7 +111,11 @@ def tile_list_stay_tension_survey_kernel(
         before = {}
 
         def gather_before(c):
-            before[c] = ring.tile([P, M], F32, name="before", tag="before", bufs=4)
+            if c == 0:
+                pair = ring.tile([P, 2, M], F32, name="before_pair", tag="big1", bufs=1, align_bytes=64)
+                before[0], before[1] = pair[:, 0, :], pair[:, 1, :]
+            elif c >= 2:
+                before[c] = ring.tile([P, M], F32, name="before", tag="before", bufs=4)
             nc.vector.tensor_copy(before[c][:], pages[c][:].indirect(idx_before[:]))
 
         w1_bf = {}
@@ -115,7 +125,7 @@ def tile_list_stay_tension_survey_kernel(
             w1_bf[c] = ring.tile([P, PASSES, P, 4], BF16, name="w1_bf", tag="w1_bf", align_bytes=64)
             nc.scalar.copy(
                 w1_bf[c][:].rearrange("p a (g i) j -> p a g j i", i=4),
-                w1_raw[c][:].rearrange("p a j (g i) -> p a g j i", i=4),
+                w1_raw[c].rearrange("p a j (g i) -> p a g j i", i=4),
             )
 
         def quantise_w1(c):
@@ -124,7 +134,6 @@ def tile_list_stay_tension_survey_kernel(
             nc.vector.quantize_mx(codes[:].bitcast(FP8X4), scales[:], w1_bf[c][:].rearrange("p a r j -> p (a r j)"))
             w1_q[c] = (codes, scales)
 
-        gather_before(0)
         round_w1(0)
         quantise_w1(0)
         v_sc = keep.tile([P, S], U8, name="v_sc", align_bytes=64)
@@ -138,18 +147,19 @@ def tile_list_stay_tension_survey_kernel(
         nc.vector.tensor_scalar(cols[:, 2, :], cols[:, 1, :], 1.0, 1.0, ALU.mult, ALU.add)
         nc.vector.tensor_scalar(cols[:, 3, :], cols[:, 1, :], -1.0, 1.0, ALU.mult, ALU.add)
 
-        nc.vector.tensor_copy(w2_sc[:], w2_sc_raw[:].rearrange("p a (q t) -> p a t q", t=4))
         for h in range(2):
             nc.vector.tensor_copy(
                 v_codes[1][:, h * BANK:(h + 1) * BANK], tab[1][:].bitcast(U32).indirect(idx_tab[:, h * 32:(h + 1) * 32])
             )
+
+        gather_before(0)
 
         h_rows = {}
 
         def make_h(c):
             codes, scales = w1_q[c]
             h_rows[c] = ring.tile([P, S], F32, name="h_rows", tag="h_rows", bufs=3)
-            a_t = ring.tile([P, S], F32, name="a_t", tag="a_t")
+            a_t = ring.tile([P, S], F32, name="a_t", tag="shared%d" % (c % 2), bufs=1)
             tanh_t = ring.tile([P, S], F32, name="tanh_t", tag="tanh_t")
             for h in range(2):
                 half = slice(h * BANK, (h + 1) * BANK)
@@ -177,19 +187,39 @@ def tile_list_stay_tension_survey_kernel(
                         )
                 nc.scalar.activation(h_rows[c][:, half], total[:], ACT.Copy, scale=cols[:, 0, c:c + 1])
 
-        def put(c, pieces):
+        def make_first_h():
+            codes, scales = w1_q[0]
+            h_rows[0] = ring.tile([P, S], F32, name="h_rows", tag="h_rows", bufs=3)
+            tanh_r = ring.tile([P, S], F32, name="tanh_r", tag="tanh_t")
+            gained = ring.tile([P, S], F32, name="gained", tag="term_d")
+            nc.scalar.activation(gained[:], wgs_sb[:], ACT.Copy, scale=cols[:, 0, 0:1])
+            for h in range(2):
+                half = slice(h * BANK, (h + 1) * BANK)
+                acc = bank("a")
+                for a in range(PASSES):
+                    nc.tensor.matmul_mx(
+                        acc[:],
+                        lhsT=codes[:, a * P:(a + 1) * P].bitcast(FP8X4), lhsT_scale=scales[:, a * P:(a + 1) * P],
+                        rhs=v_codes[a][:, half].bitcast(FP8X4), rhs_scale=v_sc[4 * a:P, half],
+                        start=(a == 0), stop=(a == PASSES - 1),
+                    )
+                nc.scalar.activation(tanh_r[:, half], acc[:], ACT.Tanh)
+                nc.vector.tensor_tensor(h_rows[0][:, half], acc[:], tanh_r[:, half], ALU.add)
+            return gained
+
+        def put(c, pieces, weight):
             n = S // pieces
             for h in range(pieces):
                 nc.vector.tensor_tensor(
                     pages[c][:].indirect(idx_put[:, h * n // 16:(h + 1) * n // 16]),
-                    h_rows[c][:, h * n:(h + 1) * n], wgs_sb[:, h * n:(h + 1) * n], ALU.mult,
+                    h_rows[c][:, h * n:(h + 1) * n], weight[:, h * n:(h + 1) * n], ALU.mult,
                 )
 
         diff = {}
 
         def gather_diff(c, m0, m1):
             if m0 == 0:
-                diff[c] = ring.tile([P, M], F32, name="diff", tag="diff")
+                diff[c] = ring.tile([P, M], F32, name="diff", tag="shared%d" % ((c + 1) % 2), bufs=1)
             nc.vector.tensor_tensor(
                 diff[c][:, m0:m1], pages[c][:].indirect(idx_after[:, m0 // 16:m1 // 16]), before[c][:, m0:m1], ALU.subtract
             )
@@ -218,7 +248,7 @@ def tile_list_stay_tension_survey_kernel(
         def sum_terms(c, m0, m1):
             b, cl = divmod(c, 4)
             if b not in x_t:
-                x_t[b] = ring.tile([P, M // P, 2, P, 2], BF16, name="x_t", tag="big", align_bytes=64)
+                x_t[b] = ring.tile([P, M // P, 2, P, 2], BF16, name="x_t", tag="big%d" % b, bufs=1, align_bytes=64)
             blocks = (m1 - m0) // P
             total = bank("xs")
             for l in range(blocks):
@@ -233,18 +263,45 @@ def tile_list_stay_tension_survey_kernel(
                 total[:, 0:blocks * P].rearrange("m (l q u e) -> m l u q e", u=2, e=2, q=32),
             )
 
+        last_x = keep.tile([P, M], BF16, name="last_x")
+
+        last_d = {}
+
+        def last_diff(c, m0, m1):
+            last_d[m0] = ring.tile([P, m1 - m0], F32, name="last_d", tag="last_d")
+            nc.vector.tensor_tensor(
+                last_d[m0][:], pages[c][:].indirect(idx_after[:, m0 // 16:m1 // 16]), before[c][:, m0:m1], ALU.subtract
+            )
+
+        def last_linear(c, m0, m1):
+            nc.vector.tensor_scalar(last_r[:, m0:m1], last_d[m0][:], 0.0, cols[:, 3, c:c + 1], ALU.max, ALU.mult)
+            nc.vector.scalar_tensor_tensor(
+                last_s[:, m0:m1], last_d[m0][:], cols[:, 1, c:c + 1], term_e[c][:, m0:m1], ALU.mult, ALU.add
+            )
+
+        def last_sum(c, m0, m1):
+            nc.vector.tensor_tensor(last_x[:, m0:m1], last_r[:, m0:m1], last_s[:, m0:m1], ALU.add)
+            blocks = (m1 - m0) // P
+            turned = psum.tile([P, blocks * P], BF16, name="xs_bf", tag="xs")
+            for l in range(blocks):
+                nc.tensor.transpose(turned[:, l * P:(l + 1) * P], last_x[:, m0 + l * P:m0 + (l + 1) * P], ident_bf[:])
+            nc.scalar.copy(
+                x_t[1][:, m0 // P:m1 // P, :, 96:128, :],
+                turned[:].rearrange("m (l q u e) -> m l u q e", u=2, e=2, q=32),
+            )
+
         x_codes = [keep.tile([P, M], U32, name="x_codes%d" % b, align_bytes=64) for b in range(PASSES)]
         x_sc = [keep.tile([P, M], U8, name="x_sc%d" % b, align_bytes=64) for b in range(PASSES)]
         x_bf = {}
 
-        def turn_x(b, g):
+        def turn_x(b, g, copy):
             words = x_t[b][:].rearrange("m l u p e -> m (l u p e)").bitcast(F32)
             turned = bank("wd")
             for i in range(4):
                 w0 = (4 * g + i) * P
                 nc.tensor.transpose(turned[:, i * P:(i + 1) * P], words[:, w0:w0 + P], ident[:])
             x_bf[b, g] = ring.tile([P, CHUNK * 4], BF16, name="x_bf", tag="x_bf", bufs=4, align_bytes=64)
-            nc.scalar.copy(
+            copy(
                 x_bf[b, g][:].bitcast(F32).rearrange("p (l m u) -> p l m u", l=2, u=2),
                 turned[:].rearrange("p (l u m) -> p l m u", l=2, u=2),
             )
@@ -260,20 +317,26 @@ def tile_list_stay_tension_survey_kernel(
         y_sb = {}
         y_bf = {}
 
-        def make_y(g):
+        y_acc = {}
+
+        def y_pass(g, b):
             m = slice(g * CHUNK, (g + 1) * CHUNK)
-            y_sb[g] = ring.tile([P, 4, CHUNK], F32, name="y_sb", tag="y_sb", bufs=3)
             for h in range(2):
-                acc = bank(("a", "u")[h])
+                if b == 0:
+                    y_acc[g, h] = bank(("a", "u")[h])
                 for i in range(2):
-                    for b in range(PASSES):
-                        nc.tensor.matmul_mx(
-                            acc[:, i * CHUNK:(i + 1) * CHUNK],
-                            lhsT=w2_codes[:, b, 2 * h + i, :].bitcast(FP4X4), lhsT_scale=w2_sc[:, b, 2 * h + i, :],
-                            rhs=x_codes[b][:, m].bitcast(FP8X4), rhs_scale=x_sc[b][:, m],
-                            start=(b == 0), stop=(b == PASSES - 1),
-                        )
-                nc.scalar.copy(y_sb[g][:, 2 * h:2 * h + 2, :], acc[:].rearrange("p (i m) -> p i m", i=2))
+                    nc.tensor.matmul_mx(
+                        y_acc[g, h][:, i * CHUNK:(i + 1) * CHUNK],
+                        lhsT=w2_codes[:, b, 2 * h + i, :].bitcast(FP4X4), lhsT_scale=w2_sc[:, b, 2 * h + i, :],
+                        rhs=x_codes[b][:, m].bitcast(FP8X4), rhs_scale=x_sc[b][:, m],
+                        start=(b == 0 and i == 0), stop=(b == PASSES - 1 and i == 1),
+                    )
+
+        def store_y(g):
+            m = slice(g * CHUNK, (g + 1) * CHUNK)
+            y_sb[g] = ring.tile([P, 4, CHUNK], F32, name="y_sb", tag="before", bufs=4)
+            for h in range(2):
+                nc.scalar.copy(y_sb[g][:, 2 * h:2 * h + 2, :], y_acc[g, h][:].rearrange("p (i m) -> p i m", i=2))
             nc.sync.dma_start(y_view[:, :, m], y_sb[g][:])
 
         def round_y(g):
@@ -287,7 +350,7 @@ def tile_list_stay_tension_survey_kernel(
             nc.vector.quantize_mx(y_codes[:, m].bitcast(FP8X4), y_sc[:, m], y_bf[g][:].rearrange("p m t -> p (m t)"))
             nc.sync.dma_start(y_words[:, m], y_codes[:, m].bitcast(I32))
 
-        make_h(0)
+        gained_wgs = make_first_h()
         round_w1(1)
         quantise_w1(1)
         gather_before(1)
@@ -295,47 +358,60 @@ def tile_list_stay_tension_survey_kernel(
         round_w1(2)
         last = SLICES - 1
         for c in range(SLICES):
-            if c + 3 < SLICES:
+            if 4 <= c + 3 < SLICES:
                 load_page(c + 3)
-                load_w1(c + 3)
-            put(c, 2 if c == 0 else 1)
+            put(c, 1, gained_wgs if c == 0 else wgs_sb)
             if c + 2 < SLICES:
                 quantise_w1(c + 2)
                 gather_before(c + 2)
+            if c == 1:
+                nc.vector.tensor_copy(w2_sc[:], w2_sc_raw[:].rearrange("p a (q t) -> p a t q", t=4))
             if c == 5:
                 for g in range(CHUNKS):
                     quantise_x(0, g)
             if c < last:
                 gather_diff(c, 0, M)
             if c >= 1:
-                diff_terms(c - 1, 0, M, False)
+                if c < last:
+                    diff_terms(c - 1, 0, M, False)
                 for h in range(2):
+                    if c == last:
+                        diff_terms(c - 1, h * BANK, (h + 1) * BANK, False)
                     sum_terms(c - 1, h * BANK, (h + 1) * BANK)
             if c == 4:
                 for g in range(CHUNKS):
-                    turn_x(0, g)
+                    turn_x(0, g, nc.scalar.copy)
             scale_before(c)
             if c + 2 < SLICES:
                 make_h(c + 2)
             if c + 3 < SLICES:
                 round_w1(c + 3)
 
-        for step in range(CHUNKS + 4):
+        last_r = ring.tile([P, M], F32, name="last_r", tag="term_r")
+        last_s = ring.tile([P, M], F32, name="last_s", tag="term_d")
+        y_pass(0, 0)
+        y_pass(1, 0)
+        for step in range(CHUNKS + 5 + 1):
             if step < CHUNKS:
-                gather_diff(last, step * CHUNK, (step + 1) * CHUNK)
+                last_diff(last, step * CHUNK, (step + 1) * CHUNK)
             g = step - 1
             if 0 <= g < CHUNKS:
-                diff_terms(last, g * CHUNK, (g + 1) * CHUNK, True)
-                sum_terms(last, g * CHUNK, (g + 1) * CHUNK)
-                turn_x(1, g)
+                last_linear(last, g * CHUNK, (g + 1) * CHUNK)
             g = step - 2
             if 0 <= g < CHUNKS:
-                quantise_x(1, g)
-                make_y(g)
+                last_sum(last, g * CHUNK, (g + 1) * CHUNK)
+                turn_x(1, g, nc.scalar.copy if g < 2 else nc.vector.tensor_copy)
             g = step - 3
             if 0 <= g < CHUNKS:
-                round_y(g)
+                quantise_x(1, g)
+                y_pass(g, 1)
+                store_y(g)
+                if g + 2 < CHUNKS:
+                    y_pass(g + 2, 0)
             g = step - 4
+            if 0 <= g < CHUNKS:
+                round_y(g)
+            g = step - 5
             if 0 <= g < CHUNKS:
                 quantise_y(g)
 

@@ -51,8 +51,6 @@ def tile_list_stay_tension_survey_kernel(
         nc.vector.memset(rows[:], 0.0)
         ident = keep.tile([P, P], F32, name="ident")
         make_identity(nc, ident[:])
-        ident_bf = keep.tile([P, P], BF16, name="ident_bf")
-        make_identity(nc, ident_bf[:])
 
         pages = {}
         w1_raw = {}
@@ -142,10 +140,11 @@ def tile_list_stay_tension_survey_kernel(
         nc.vector.tensor_copy(v_codes[0][:], tab[0][:].bitcast(U32).indirect(idx_tab[:]))
         cols_ps = bank("wd")
         nc.tensor.transpose(cols_ps[:, 0:P], rows[:], ident[:])
-        cols = keep.tile([P, 4, SLICES], F32, name="cols")
+        cols = keep.tile([P, 5, SLICES], F32, name="cols")
         nc.vector.tensor_copy(cols[:, 0:2, :], cols_ps[:, 0:2 * SLICES].rearrange("p (k c) -> p k c", k=2))
         nc.vector.tensor_scalar(cols[:, 2, :], cols[:, 1, :], 1.0, 1.0, ALU.mult, ALU.add)
         nc.vector.tensor_scalar(cols[:, 3, :], cols[:, 1, :], -1.0, 1.0, ALU.mult, ALU.add)
+        nc.vector.tensor_scalar(cols[:, 4, :], cols[:, 1, :], 1.0, -1.0, ALU.mult, ALU.add)
 
         for h in range(2):
             nc.vector.tensor_copy(
@@ -191,7 +190,7 @@ def tile_list_stay_tension_survey_kernel(
             codes, scales = w1_q[0]
             h_rows[0] = ring.tile([P, S], F32, name="h_rows", tag="h_rows", bufs=3)
             tanh_r = ring.tile([P, S], F32, name="tanh_r", tag="tanh_t")
-            gained = ring.tile([P, S], F32, name="gained", tag="term_d")
+            gained = ring.tile([P, S], F32, name="gained", tag="term_r")
             nc.scalar.activation(gained[:], wgs_sb[:], ACT.Copy, scale=cols[:, 0, 0:1])
             for h in range(2):
                 half = slice(h * BANK, (h + 1) * BANK)
@@ -225,69 +224,73 @@ def tile_list_stay_tension_survey_kernel(
             )
 
         term_e = {}
-        term_d = {}
         term_r = {}
 
         def scale_before(c):
             term_e[c] = ring.tile([P, M], F32, name="term_e", tag="term_e")
             nc.scalar.activation(term_e[c][:], before[c][:], ACT.Copy, scale=cols[:, 2, c:c + 1])
 
-        def diff_terms(c, m0, m1, on_vector):
+        def diff_terms(c, m0, m1):
             if m0 == 0:
-                term_d[c] = ring.tile([P, M], F32, name="term_d", tag="term_d")
                 term_r[c] = ring.tile([P, M], F32, name="term_r", tag="term_r")
-            nc.scalar.activation(term_d[c][:, m0:m1], diff[c][:, m0:m1], ACT.Copy, scale=cols[:, 1, c:c + 1])
-            if on_vector:
-                nc.vector.tensor_scalar(term_r[c][:, m0:m1], diff[c][:, m0:m1], 0.0, cols[:, 3, c:c + 1], ALU.max, ALU.mult)
-            else:
-                nc.scalar.activation(term_r[c][:, m0:m1], diff[c][:, m0:m1], ACT.Relu)
-                nc.scalar.activation(term_r[c][:, m0:m1], term_r[c][:, m0:m1], ACT.Copy, scale=cols[:, 3, c:c + 1])
+            nc.scalar.activation(term_r[c][:, m0:m1], diff[c][:, m0:m1], ACT.Relu, scale=-1.0)
+            nc.scalar.activation(term_r[c][:, m0:m1], term_r[c][:, m0:m1], ACT.Copy, scale=cols[:, 3, c:c + 1])
 
         x_t = {}
 
+        def x_t_tiles(b):
+            if b == 0:
+                whole = ring.tile([P, CHUNKS, 2, 2, P, 2], BF16, name="x_t", tag="big0", bufs=1, align_bytes=64)
+                for g in range(CHUNKS):
+                    x_t[0, g] = whole[:, g]
+                x_t[0] = whole[:].rearrange("m g l u p e -> m (g l) u p e")
+            else:
+                for g in range(CHUNKS):
+                    x_t[1, g] = keep.tile([P, 2, 2, P, 2], BF16, name="x_t1_%d" % g)[:]
+
         def sum_terms(c, m0, m1):
             b, cl = divmod(c, 4)
-            if b not in x_t:
-                x_t[b] = ring.tile([P, M // P, 2, P, 2], BF16, name="x_t", tag="big%d" % b, bufs=1, align_bytes=64)
+            if (b, 0) not in x_t:
+                x_t_tiles(b)
             blocks = (m1 - m0) // P
             total = bank("xs")
             for l in range(blocks):
                 m = slice(m0 + l * P, m0 + (l + 1) * P)
                 for term in range(3):
                     nc.tensor.matmul(
-                        total[:, l * P:(l + 1) * P], lhsT=(term_e, term_d, term_r)[term][c][:, m], rhs=ident[:],
+                        total[:, l * P:(l + 1) * P], lhsT=(term_e, diff, term_r)[term][c][:, m], rhs=ident[:],
+                        start=(term == 0), stop=(term == 2), is_transpose=True,
+                    )
+            rounded = total[:].rearrange("m (l q u e) -> m l u q e", u=2, e=2, q=32)
+            if b == 0:
+                nc.scalar.copy(x_t[0][:, m0 // P:m1 // P, :, 32 * cl:32 * (cl + 1), :], rounded)
+            else:
+                for i in range(2):
+                    nc.scalar.copy(x_t[1, m0 // CHUNK + i][:, :, :, 32 * cl:32 * (cl + 1), :], rounded[:, 2 * i:2 * i + 2])
+
+        def last_diff(c, g):
+            m = slice(g * CHUNK, (g + 1) * CHUNK)
+            nc.vector.tensor_tensor(
+                last_d[:, m], pages[c][:].indirect(idx_after[:, g * CHUNK // 16:(g + 1) * CHUNK // 16]), before[c][:, m],
+                ALU.subtract,
+            )
+
+        def last_term(c, g):
+            m = slice(g * CHUNK, (g + 1) * CHUNK)
+            nc.vector.tensor_scalar(last_r[:, m], last_d[:, m], 0.0, cols[:, 4, c:c + 1], ALU.min, ALU.mult)
+
+        def last_sum(c, g):
+            total = bank("xs")
+            for l in range(2):
+                m = slice(g * CHUNK + l * P, g * CHUNK + (l + 1) * P)
+                for term in range(3):
+                    nc.tensor.matmul(
+                        total[:, l * P:(l + 1) * P], lhsT=(term_e[c], last_d, last_r)[term][:, m], rhs=ident[:],
                         start=(term == 0), stop=(term == 2), is_transpose=True,
                     )
             nc.scalar.copy(
-                x_t[b][:, m0 // P:m1 // P, :, 32 * cl:32 * (cl + 1), :],
-                total[:, 0:blocks * P].rearrange("m (l q u e) -> m l u q e", u=2, e=2, q=32),
-            )
-
-        last_x = keep.tile([P, M], BF16, name="last_x")
-
-        last_d = {}
-
-        def last_diff(c, m0, m1):
-            last_d[m0] = ring.tile([P, m1 - m0], F32, name="last_d", tag="last_d")
-            nc.vector.tensor_tensor(
-                last_d[m0][:], pages[c][:].indirect(idx_after[:, m0 // 16:m1 // 16]), before[c][:, m0:m1], ALU.subtract
-            )
-
-        def last_linear(c, m0, m1):
-            nc.vector.tensor_scalar(last_r[:, m0:m1], last_d[m0][:], 0.0, cols[:, 3, c:c + 1], ALU.max, ALU.mult)
-            nc.vector.scalar_tensor_tensor(
-                last_s[:, m0:m1], last_d[m0][:], cols[:, 1, c:c + 1], term_e[c][:, m0:m1], ALU.mult, ALU.add
-            )
-
-        def last_sum(c, m0, m1):
-            nc.vector.tensor_tensor(last_x[:, m0:m1], last_r[:, m0:m1], last_s[:, m0:m1], ALU.add)
-            blocks = (m1 - m0) // P
-            turned = psum.tile([P, blocks * P], BF16, name="xs_bf", tag="xs")
-            for l in range(blocks):
-                nc.tensor.transpose(turned[:, l * P:(l + 1) * P], last_x[:, m0 + l * P:m0 + (l + 1) * P], ident_bf[:])
-            nc.scalar.copy(
-                x_t[1][:, m0 // P:m1 // P, :, 96:128, :],
-                turned[:].rearrange("m (l q u e) -> m l u q e", u=2, e=2, q=32),
+                x_t[1, g][:, :, :, 96:128, :],
+                total[:, 0:CHUNK].rearrange("m (l q u e) -> m l u q e", u=2, e=2, q=32),
             )
 
         x_codes = [keep.tile([P, M], U32, name="x_codes%d" % b, align_bytes=64) for b in range(PASSES)]
@@ -295,11 +298,10 @@ def tile_list_stay_tension_survey_kernel(
         x_bf = {}
 
         def turn_x(b, g, copy):
-            words = x_t[b][:].rearrange("m l u p e -> m (l u p e)").bitcast(F32)
+            words = x_t[b, g].rearrange("m l u p e -> m (l u p e)").bitcast(F32)
             turned = bank("wd")
             for i in range(4):
-                w0 = (4 * g + i) * P
-                nc.tensor.transpose(turned[:, i * P:(i + 1) * P], words[:, w0:w0 + P], ident[:])
+                nc.tensor.transpose(turned[:, i * P:(i + 1) * P], words[:, i * P:(i + 1) * P], ident[:])
             x_bf[b, g] = ring.tile([P, CHUNK * 4], BF16, name="x_bf", tag="x_bf", bufs=4, align_bytes=64)
             copy(
                 x_bf[b, g][:].bitcast(F32).rearrange("p (l m u) -> p l m u", l=2, u=2),
@@ -373,10 +375,10 @@ def tile_list_stay_tension_survey_kernel(
                 gather_diff(c, 0, M)
             if c >= 1:
                 if c < last:
-                    diff_terms(c - 1, 0, M, False)
+                    diff_terms(c - 1, 0, M)
                 for h in range(2):
                     if c == last:
-                        diff_terms(c - 1, h * BANK, (h + 1) * BANK, False)
+                        diff_terms(c - 1, h * BANK, (h + 1) * BANK)
                     sum_terms(c - 1, h * BANK, (h + 1) * BANK)
             if c == 4:
                 for g in range(CHUNKS):
@@ -388,18 +390,18 @@ def tile_list_stay_tension_survey_kernel(
                 round_w1(c + 3)
 
         last_r = ring.tile([P, M], F32, name="last_r", tag="term_r")
-        last_s = ring.tile([P, M], F32, name="last_s", tag="term_d")
+        last_d = ring.tile([P, M], F32, name="last_d", tag="tanh_t")
         y_pass(0, 0)
         y_pass(1, 0)
-        for step in range(CHUNKS + 5 + 1):
+        for step in range(CHUNKS + 5):
             if step < CHUNKS:
-                last_diff(last, step * CHUNK, (step + 1) * CHUNK)
+                last_diff(last, step)
             g = step - 1
             if 0 <= g < CHUNKS:
-                last_linear(last, g * CHUNK, (g + 1) * CHUNK)
+                last_term(last, g)
+                last_sum(last, g)
             g = step - 2
             if 0 <= g < CHUNKS:
-                last_sum(last, g * CHUNK, (g + 1) * CHUNK)
                 turn_x(1, g, nc.scalar.copy if g < 2 else nc.vector.tensor_copy)
             g = step - 3
             if 0 <= g < CHUNKS:

@@ -72,19 +72,19 @@ def tile_list_stay_tension_survey_kernel(
         def load_tab(a):
             nc.sync.dma_start(tab[a][:], tab_words[a].rearrange("p t i -> p (t i)").bitcast(I32))
 
-        for tile, lists in ((idx_tab, offs), (idx_before, offs4), (idx_put, offs2), (idx_after, offs3)):
-            nc.sync.dma_start(tile[:], lists)
+        nc.sync.dma_start(idx_tab[:], offs)
         load_tab(0)
         load_w1(0, 1)
         w2_raw = keep.tile([P, PASSES, 2 * N], U8, name="w2_raw")
         nc.sync.dma_start(w2_raw[:].bitcast(I32), w2_words.rearrange("a p n -> p a n").bitcast(I32))
-        for q in range(4):
-            nc.sync.dma_start(tab_sc[32 * q:32 * q + 8, :].bitcast(I32), tab_scales[:, 4 * q:4 * q + 4, :].bitcast(I32))
         load_tab(1)
+        nc.sync.dma_start(idx_before[:], offs4)
         load_page(0)
         wgs_sb = keep.tile([P, S], F32, name="wgs_sb")
         nc.sync.dma_start(wgs_sb[:], wgs)
+        nc.sync.dma_start(idx_put[:], offs2)
         load_w1(1, 2)
+        nc.sync.dma_start(idx_after[:], offs3)
         load_page(1)
         load_page(2)
         load_w1(2, 4)
@@ -96,6 +96,8 @@ def tile_list_stay_tension_survey_kernel(
         load_page(3)
         load_w1(4, 8)
 
+        for q in range(4):
+            nc.gpsimd.dma_start(tab_sc[32 * q:32 * q + 8, :].bitcast(I32), tab_scales[:, 4 * q:4 * q + 4, :].bitcast(I32))
         nc.gpsimd.dma_start(rows[0:SLICES, :], gain.rearrange("(c p) -> c p", p=P))
         nc.gpsimd.dma_start(rows[SLICES:2 * SLICES, :], low.rearrange("(c p) -> c p", p=P))
 
@@ -155,36 +157,49 @@ def tile_list_stay_tension_survey_kernel(
 
         h_rows = {}
 
-        def make_h(c):
+        a_acc = {}
+        a_t = {}
+        tanh_t = {}
+        h_acc = {}
+
+        def first_product(c):
             codes, scales = w1_q[c]
-            h_rows[c] = ring.tile([P, S], F32, name="h_rows", tag="h_rows", bufs=3)
-            a_t = ring.tile([P, S], F32, name="a_t", tag="shared%d" % (c % 2), bufs=1)
-            tanh_t = ring.tile([P, S], F32, name="tanh_t", tag="tanh_t")
             for h in range(2):
-                half = slice(h * BANK, (h + 1) * BANK)
-                acc = bank("a")
+                a_acc[c, h] = bank("a")
                 for b in range(4):
                     j = slice(h * BANK + b * P, h * BANK + (b + 1) * P)
                     for a in range(PASSES):
                         nc.tensor.matmul_mx(
-                            acc[:, b * P:(b + 1) * P],
+                            a_acc[c, h][:, b * P:(b + 1) * P],
                             lhsT=v_codes[a][:, j].bitcast(FP8X4), lhsT_scale=v_sc[4 * a:P, j],
                             rhs=codes[:, a * P:(a + 1) * P].bitcast(FP8X4), rhs_scale=scales[:, a * P:(a + 1) * P],
                             start=(a == 0), stop=(a == PASSES - 1),
                         )
-                nc.scalar.activation(tanh_t[:, half], acc[:], ACT.Tanh)
-                nc.scalar.copy(a_t[:, half], acc[:])
+
+        def read_product(c):
+            a_t[c] = ring.tile([P, S], F32, name="a_t", tag="shared%d" % (c % 2), bufs=1)
+            tanh_t[c] = ring.tile([P, S], F32, name="tanh_t", tag="tanh_t")
             for h in range(2):
                 half = slice(h * BANK, (h + 1) * BANK)
-                total = bank("u")
+                nc.scalar.activation(tanh_t[c][:, half], a_acc[c, h][:], ACT.Tanh)
+                nc.scalar.copy(a_t[c][:, half], a_acc[c, h][:])
+
+        def add_tanh(c):
+            for h in range(2):
+                h_acc[c, h] = bank("u")
                 for b in range(4):
                     j = slice(h * BANK + b * P, h * BANK + (b + 1) * P)
                     for term in (0, 1):
                         nc.tensor.matmul(
-                            total[:, b * P:(b + 1) * P], lhsT=(tanh_t, a_t)[term][:, j], rhs=ident[:],
+                            h_acc[c, h][:, b * P:(b + 1) * P], lhsT=(tanh_t, a_t)[term][c][:, j], rhs=ident[:],
                             start=(term == 0), stop=(term == 1), is_transpose=True,
                         )
-                nc.scalar.activation(h_rows[c][:, half], total[:], ACT.Copy, scale=cols[:, 0, c:c + 1])
+
+        def scale_h(c):
+            h_rows[c] = ring.tile([P, S], F32, name="h_rows", tag="h_rows", bufs=3)
+            for h in range(2):
+                half = slice(h * BANK, (h + 1) * BANK)
+                nc.scalar.activation(h_rows[c][:, half], h_acc[c, h][:], ACT.Copy, scale=cols[:, 0, c:c + 1])
 
         def make_first_h():
             codes, scales = w1_q[0]
@@ -237,6 +252,7 @@ def tile_list_stay_tension_survey_kernel(
             nc.scalar.activation(term_r[c][:, m0:m1], term_r[c][:, m0:m1], ACT.Copy, scale=cols[:, 3, c:c + 1])
 
         x_t = {}
+        x_acc = {}
 
         def x_t_tiles(b):
             if b == 0:
@@ -261,7 +277,11 @@ def tile_list_stay_tension_survey_kernel(
                         total[:, l * P:(l + 1) * P], lhsT=(term_e, diff, term_r)[term][c][:, m], rhs=ident[:],
                         start=(term == 0), stop=(term == 2), is_transpose=True,
                     )
-            rounded = total[:].rearrange("m (l q u e) -> m l u q e", u=2, e=2, q=32)
+            x_acc[c, m0] = total
+
+        def round_x(c, m0, m1):
+            b, cl = divmod(c, 4)
+            rounded = x_acc[c, m0][:].rearrange("m (l q u e) -> m l u q e", u=2, e=2, q=32)
             if b == 0:
                 nc.scalar.copy(x_t[0][:, m0 // P:m1 // P, :, 32 * cl:32 * (cl + 1), :], rounded)
             else:
@@ -297,15 +317,20 @@ def tile_list_stay_tension_survey_kernel(
         x_sc = [keep.tile([P, M], U8, name="x_sc%d" % b, align_bytes=64) for b in range(PASSES)]
         x_bf = {}
 
-        def turn_x(b, g, copy):
+        x_turned = {}
+
+        def turn_x(b, g):
             words = x_t[b, g].rearrange("m l u p e -> m (l u p e)").bitcast(F32)
             turned = bank("wd")
             for i in range(4):
                 nc.tensor.transpose(turned[:, i * P:(i + 1) * P], words[:, i * P:(i + 1) * P], ident[:])
+            x_turned[b, g] = turned
+
+        def weave_x(b, g, copy):
             x_bf[b, g] = ring.tile([P, CHUNK * 4], BF16, name="x_bf", tag="x_bf", bufs=4, align_bytes=64)
             copy(
                 x_bf[b, g][:].bitcast(F32).rearrange("p (l m u) -> p l m u", l=2, u=2),
-                turned[:].rearrange("p (l u m) -> p l m u", l=2, u=2),
+                x_turned[b, g][:].rearrange("p (l u m) -> p l m u", l=2, u=2),
             )
 
         def quantise_x(b, g):
@@ -355,41 +380,54 @@ def tile_list_stay_tension_survey_kernel(
         gained_wgs = make_first_h()
         round_w1(1)
         quantise_w1(1)
+        first_product(1)
         gather_before(1)
-        make_h(1)
+        read_product(1)
+        add_tanh(1)
         round_w1(2)
+        quantise_w1(2)
+        scale_h(1)
+        first_product(2)
         last = SLICES - 1
+        halves = [(h * BANK, (h + 1) * BANK) for h in range(2)]
         for c in range(SLICES):
             if 4 <= c + 3 < SLICES:
                 load_page(c + 3)
             put(c, 1, gained_wgs if c == 0 else wgs_sb)
             if c + 2 < SLICES:
-                quantise_w1(c + 2)
                 gather_before(c + 2)
             if c == 1:
                 nc.vector.tensor_copy(w2_sc[:], w2_sc_raw[:].rearrange("p a (q t) -> p a t q", t=4))
-            if c == 5:
-                for g in range(CHUNKS):
-                    quantise_x(0, g)
             if c < last:
                 gather_diff(c, 0, M)
             if c >= 1:
-                if c < last:
-                    diff_terms(c - 1, 0, M)
-                for h in range(2):
-                    if c == last:
-                        diff_terms(c - 1, h * BANK, (h + 1) * BANK)
-                    sum_terms(c - 1, h * BANK, (h + 1) * BANK)
-            if c == 4:
-                for g in range(CHUNKS):
-                    turn_x(0, g, nc.scalar.copy)
-            scale_before(c)
+                for m0, m1 in (halves if c == last else [(0, M)]):
+                    diff_terms(c - 1, m0, m1)
+                for m0, m1 in halves:
+                    sum_terms(c - 1, m0, m1)
             if c + 2 < SLICES:
-                make_h(c + 2)
+                read_product(c + 2)
+                add_tanh(c + 2)
+            if c in (5, 6):
+                for g in (2 * c - 10, 2 * c - 9):
+                    weave_x(0, g, nc.scalar.copy)
+                    quantise_x(0, g)
+            scale_before(c)
             if c + 3 < SLICES:
                 round_w1(c + 3)
+                quantise_w1(c + 3)
+            if c >= 1:
+                for m0, m1 in halves:
+                    round_x(c - 1, m0, m1)
+            if c + 2 < SLICES:
+                scale_h(c + 2)
+            if c + 3 < SLICES:
+                first_product(c + 3)
+            if c in (4, 5):
+                for g in (2 * c - 8, 2 * c - 7):
+                    turn_x(0, g)
 
-        last_r = ring.tile([P, M], F32, name="last_r", tag="term_r")
+        last_r = ring.tile([P, M], F32, name="last_r", tag="h_rows", bufs=3)
         last_d = ring.tile([P, M], F32, name="last_d", tag="tanh_t")
         y_pass(0, 0)
         y_pass(1, 0)
@@ -402,7 +440,8 @@ def tile_list_stay_tension_survey_kernel(
                 last_sum(last, g)
             g = step - 2
             if 0 <= g < CHUNKS:
-                turn_x(1, g, nc.scalar.copy if g < 2 else nc.vector.tensor_copy)
+                turn_x(1, g)
+                weave_x(1, g, nc.scalar.copy if g < 2 else nc.vector.tensor_copy)
             g = step - 3
             if 0 <= g < CHUNKS:
                 quantise_x(1, g)

@@ -19,10 +19,17 @@ ACT = mybir.ActivationFunctionType
 
 P = 128
 BANK = 512
+STRIPE = 16
 SLICES = H // P
 PASSES = 2
+PER_PASS = SLICES // PASSES
+QUAD = P // PER_PASS
+LAST = SLICES - 1
 CHUNK = 256
 CHUNKS = M // CHUNK
+TENSOR_CHUNKS = 2
+GAIN, LOW, ONE_PLUS_LOW, ONE_MINUS_LOW, LOW_MINUS_ONE = range(5)
+PAGE_BUFS, BEFORE_BUFS, H_BUFS, W1_BUFS = 4, 4, 3, 3
 
 
 def tile_list_stay_tension_survey_kernel(
@@ -38,10 +45,10 @@ def tile_list_stay_tension_survey_kernel(
         def bank(tag):
             return psum.tile([P, BANK], F32, name=tag, tag=tag)
 
-        idx_tab = keep.tile([P, S // 16], U16, name="idx_tab")
-        idx_put = keep.tile([P, S // 16], U16, name="idx_put")
-        idx_after = keep.tile([P, M // 16], U16, name="idx_after")
-        idx_before = keep.tile([P, M // 16], U16, name="idx_before")
+        idx_tab = keep.tile([P, S // STRIPE], U16, name="idx_tab")
+        idx_put = keep.tile([P, S // STRIPE], U16, name="idx_put")
+        idx_after = keep.tile([P, M // STRIPE], U16, name="idx_after")
+        idx_before = keep.tile([P, M // STRIPE], U16, name="idx_before")
 
         tab_sc = keep.tile([P, T], U8, name="tab_sc", align_bytes=64)
         w2_sc_raw = keep.tile([P, PASSES, N], U8, name="w2_sc_raw")
@@ -51,12 +58,14 @@ def tile_list_stay_tension_survey_kernel(
         nc.vector.memset(rows[:], 0.0)
         ident = keep.tile([P, P], F32, name="ident")
         make_identity(nc, ident[:])
+        ident_bf = keep.tile([P, P], BF16, name="ident_bf")
+        make_identity(nc, ident_bf[:])
 
         pages = {}
         w1_raw = {}
 
         def load_page(c):
-            pages[c] = ring.tile([P, T2], F32, name="page", tag="page", bufs=4)
+            pages[c] = ring.tile([P, T2], F32, name="page", tag="page", bufs=PAGE_BUFS)
             nc.sync.dma_start(pages[c][:], page0[c * P:(c + 1) * P, :])
 
         def load_w1(c0, c1):
@@ -87,17 +96,19 @@ def tile_list_stay_tension_survey_kernel(
         nc.sync.dma_start(idx_after[:], offs3)
         load_page(1)
         load_page(2)
-        load_w1(2, 4)
+        load_w1(2, PER_PASS)
         for q in range(4):
             nc.sync.dma_start(
-                w2_sc_raw[32 * q:32 * q + 4].bitcast(I32),
+                w2_sc_raw[QUAD * q:QUAD * q + 4].bitcast(I32),
                 w2_scales[:, 4 * q:4 * q + 4, :].rearrange("a r n -> r a n").bitcast(I32),
             )
         load_page(3)
-        load_w1(4, 8)
+        load_w1(PER_PASS, SLICES)
 
         for q in range(4):
-            nc.gpsimd.dma_start(tab_sc[32 * q:32 * q + 8, :].bitcast(I32), tab_scales[:, 4 * q:4 * q + 4, :].bitcast(I32))
+            nc.gpsimd.dma_start(
+                tab_sc[QUAD * q:QUAD * q + 4 * PASSES, :].bitcast(I32), tab_scales[:, 4 * q:4 * q + 4, :].bitcast(I32)
+            )
         nc.gpsimd.dma_start(rows[0:SLICES, :], gain.rearrange("(c p) -> c p", p=P))
         nc.gpsimd.dma_start(rows[SLICES:2 * SLICES, :], low.rearrange("(c p) -> c p", p=P))
 
@@ -108,6 +119,9 @@ def tile_list_stay_tension_survey_kernel(
             w2_raw[:].rearrange("p a (q t b) -> p a t q b", t=4, b=2),
         )
 
+        def deal_w2_scales():
+            nc.vector.tensor_copy(w2_sc[:], w2_sc_raw[:].rearrange("p a (q t) -> p a t q", t=4))
+
         before = {}
 
         def gather_before(c):
@@ -115,7 +129,7 @@ def tile_list_stay_tension_survey_kernel(
                 pair = ring.tile([P, 2, M], F32, name="before_pair", tag="big1", bufs=1, align_bytes=64)
                 before[0], before[1] = pair[:, 0, :], pair[:, 1, :]
             elif c >= 2:
-                before[c] = ring.tile([P, M], F32, name="before", tag="before", bufs=4)
+                before[c] = ring.tile([P, M], F32, name="before", tag="before", bufs=BEFORE_BUFS)
             nc.vector.tensor_copy(before[c][:], pages[c][:].indirect(idx_before[:]))
 
         w1_bf = {}
@@ -129,8 +143,8 @@ def tile_list_stay_tension_survey_kernel(
             )
 
         def quantise_w1(c):
-            codes = ring.tile([P, PASSES * P], U32, name="w1_codes", tag="w1_codes", bufs=3, align_bytes=64)
-            scales = ring.tile([P, PASSES * P], U8, name="w1_scales", tag="w1_scales", bufs=3, align_bytes=64)
+            codes = ring.tile([P, PASSES * P], U32, name="w1_codes", tag="w1_codes", bufs=W1_BUFS, align_bytes=64)
+            scales = ring.tile([P, PASSES * P], U8, name="w1_scales", tag="w1_scales", bufs=W1_BUFS, align_bytes=64)
             nc.vector.quantize_mx(codes[:].bitcast(FP8X4), scales[:], w1_bf[c][:].rearrange("p a r j -> p (a r j)"))
             w1_q[c] = (codes, scales)
 
@@ -143,20 +157,22 @@ def tile_list_stay_tension_survey_kernel(
         cols_ps = bank("wd")
         nc.tensor.transpose(cols_ps[:, 0:P], rows[:], ident[:])
         cols = keep.tile([P, 5, SLICES], F32, name="cols")
-        nc.vector.tensor_copy(cols[:, 0:2, :], cols_ps[:, 0:2 * SLICES].rearrange("p (k c) -> p k c", k=2))
-        nc.vector.tensor_scalar(cols[:, 2, :], cols[:, 1, :], 1.0, 1.0, ALU.mult, ALU.add)
-        nc.vector.tensor_scalar(cols[:, 3, :], cols[:, 1, :], -1.0, 1.0, ALU.mult, ALU.add)
-        nc.vector.tensor_scalar(cols[:, 4, :], cols[:, 1, :], 1.0, -1.0, ALU.mult, ALU.add)
+        nc.vector.tensor_copy(cols[:, GAIN:LOW + 1, :], cols_ps[:, 0:2 * SLICES].rearrange("p (k c) -> p k c", k=2))
+        nc.vector.tensor_scalar(cols[:, ONE_PLUS_LOW, :], cols[:, LOW, :], 1.0, 1.0, ALU.mult, ALU.add)
+        nc.vector.tensor_scalar(cols[:, ONE_MINUS_LOW, :], cols[:, LOW, :], -1.0, 1.0, ALU.mult, ALU.add)
+        nc.vector.tensor_scalar(cols[:, LOW_MINUS_ONE, :], cols[:, LOW, :], 1.0, -1.0, ALU.mult, ALU.add)
 
-        for h in range(2):
-            nc.vector.tensor_copy(
-                v_codes[1][:, h * BANK:(h + 1) * BANK], tab[1][:].bitcast(U32).indirect(idx_tab[:, h * 32:(h + 1) * 32])
-            )
+        halves = [slice(i * BANK, (i + 1) * BANK) for i in range(2)]
+
+        def entries(tile, span):
+            return tile[:, span.start // STRIPE:span.stop // STRIPE]
+
+        for half in halves:
+            nc.vector.tensor_copy(v_codes[1][:, half], tab[1][:].bitcast(U32).indirect(entries(idx_tab, half)))
 
         gather_before(0)
 
         h_rows = {}
-
         a_acc = {}
         a_t = {}
         tanh_t = {}
@@ -164,13 +180,13 @@ def tile_list_stay_tension_survey_kernel(
 
         def first_product(c):
             codes, scales = w1_q[c]
-            for h in range(2):
-                a_acc[c, h] = bank("a")
-                for b in range(4):
-                    j = slice(h * BANK + b * P, h * BANK + (b + 1) * P)
+            for i, half in enumerate(halves):
+                a_acc[c, i] = bank("a")
+                for blk in range(4):
+                    j = slice(half.start + blk * P, half.start + (blk + 1) * P)
                     for a in range(PASSES):
                         nc.tensor.matmul_mx(
-                            a_acc[c, h][:, b * P:(b + 1) * P],
+                            a_acc[c, i][:, blk * P:(blk + 1) * P],
                             lhsT=v_codes[a][:, j].bitcast(FP8X4), lhsT_scale=v_sc[4 * a:P, j],
                             rhs=codes[:, a * P:(a + 1) * P].bitcast(FP8X4), rhs_scale=scales[:, a * P:(a + 1) * P],
                             start=(a == 0), stop=(a == PASSES - 1),
@@ -179,36 +195,35 @@ def tile_list_stay_tension_survey_kernel(
         def read_product(c):
             a_t[c] = ring.tile([P, S], F32, name="a_t", tag="shared%d" % (c % 2), bufs=1)
             tanh_t[c] = ring.tile([P, S], F32, name="tanh_t", tag="tanh_t")
-            for h in range(2):
-                half = slice(h * BANK, (h + 1) * BANK)
-                nc.scalar.activation(tanh_t[c][:, half], a_acc[c, h][:], ACT.Tanh)
-                nc.scalar.copy(a_t[c][:, half], a_acc[c, h][:])
+            for i, half in enumerate(halves):
+                nc.scalar.activation(tanh_t[c][:, half], a_acc[c, i][:], ACT.Tanh)
+                nc.scalar.copy(a_t[c][:, half], a_acc[c, i][:])
+
+        def add_turned(out, terms):
+            for i, term in enumerate(terms):
+                nc.tensor.matmul(
+                    out, lhsT=term, rhs=ident[:], start=(i == 0), stop=(i == len(terms) - 1), is_transpose=True
+                )
 
         def add_tanh(c):
-            for h in range(2):
-                h_acc[c, h] = bank("u")
-                for b in range(4):
-                    j = slice(h * BANK + b * P, h * BANK + (b + 1) * P)
-                    for term in (0, 1):
-                        nc.tensor.matmul(
-                            h_acc[c, h][:, b * P:(b + 1) * P], lhsT=(tanh_t, a_t)[term][c][:, j], rhs=ident[:],
-                            start=(term == 0), stop=(term == 1), is_transpose=True,
-                        )
+            for i, half in enumerate(halves):
+                h_acc[c, i] = bank("u")
+                for blk in range(4):
+                    j = slice(half.start + blk * P, half.start + (blk + 1) * P)
+                    add_turned(h_acc[c, i][:, blk * P:(blk + 1) * P], [tanh_t[c][:, j], a_t[c][:, j]])
 
         def scale_h(c):
-            h_rows[c] = ring.tile([P, S], F32, name="h_rows", tag="h_rows", bufs=3)
-            for h in range(2):
-                half = slice(h * BANK, (h + 1) * BANK)
-                nc.scalar.activation(h_rows[c][:, half], h_acc[c, h][:], ACT.Copy, scale=cols[:, 0, c:c + 1])
+            h_rows[c] = ring.tile([P, S], F32, name="h_rows", tag="h_rows", bufs=H_BUFS)
+            for i, half in enumerate(halves):
+                nc.scalar.activation(h_rows[c][:, half], h_acc[c, i][:], ACT.Copy, scale=cols[:, GAIN, c:c + 1])
 
-        def make_first_h():
+        def first_slice():
             codes, scales = w1_q[0]
-            h_rows[0] = ring.tile([P, S], F32, name="h_rows", tag="h_rows", bufs=3)
+            h_rows[0] = ring.tile([P, S], F32, name="h_rows", tag="h_rows", bufs=H_BUFS)
             tanh_r = ring.tile([P, S], F32, name="tanh_r", tag="tanh_t")
             gained = ring.tile([P, S], F32, name="gained", tag="term_r")
-            nc.scalar.activation(gained[:], wgs_sb[:], ACT.Copy, scale=cols[:, 0, 0:1])
-            for h in range(2):
-                half = slice(h * BANK, (h + 1) * BANK)
+            nc.scalar.activation(gained[:], wgs_sb[:], ACT.Copy, scale=cols[:, GAIN, 0:1])
+            for half in halves:
                 acc = bank("a")
                 for a in range(PASSES):
                     nc.tensor.matmul_mx(
@@ -221,163 +236,162 @@ def tile_list_stay_tension_survey_kernel(
                 nc.vector.tensor_tensor(h_rows[0][:, half], acc[:], tanh_r[:, half], ALU.add)
             return gained
 
-        def put(c, pieces, weight):
-            n = S // pieces
-            for h in range(pieces):
-                nc.vector.tensor_tensor(
-                    pages[c][:].indirect(idx_put[:, h * n // 16:(h + 1) * n // 16]),
-                    h_rows[c][:, h * n:(h + 1) * n], weight[:, h * n:(h + 1) * n], ALU.mult,
-                )
+        def put(c, weight):
+            nc.vector.tensor_tensor(pages[c][:].indirect(idx_put[:]), h_rows[c][:], weight[:], ALU.mult)
 
         diff = {}
-
-        def gather_diff(c, m0, m1):
-            if m0 == 0:
-                diff[c] = ring.tile([P, M], F32, name="diff", tag="shared%d" % ((c + 1) % 2), bufs=1)
-            nc.vector.tensor_tensor(
-                diff[c][:, m0:m1], pages[c][:].indirect(idx_after[:, m0 // 16:m1 // 16]), before[c][:, m0:m1], ALU.subtract
-            )
-
         term_e = {}
         term_r = {}
 
+        def gather_diff(c):
+            diff[c] = ring.tile([P, M], F32, name="diff", tag="shared%d" % ((c + 1) % 2), bufs=1)
+            nc.vector.tensor_tensor(diff[c][:], pages[c][:].indirect(idx_after[:]), before[c][:], ALU.subtract)
+
         def scale_before(c):
             term_e[c] = ring.tile([P, M], F32, name="term_e", tag="term_e")
-            nc.scalar.activation(term_e[c][:], before[c][:], ACT.Copy, scale=cols[:, 2, c:c + 1])
+            nc.scalar.activation(term_e[c][:], before[c][:], ACT.Copy, scale=cols[:, ONE_PLUS_LOW, c:c + 1])
 
-        def diff_terms(c, m0, m1):
-            if m0 == 0:
-                term_r[c] = ring.tile([P, M], F32, name="term_r", tag="term_r")
-            nc.scalar.activation(term_r[c][:, m0:m1], diff[c][:, m0:m1], ACT.Relu, scale=-1.0)
-            nc.scalar.activation(term_r[c][:, m0:m1], term_r[c][:, m0:m1], ACT.Copy, scale=cols[:, 3, c:c + 1])
+        def relu_term(c, spans):
+            term_r[c] = ring.tile([P, M], F32, name="term_r", tag="term_r")
+            for m in spans:
+                nc.scalar.activation(term_r[c][:, m], diff[c][:, m], ACT.Relu, scale=-1.0)
+                nc.scalar.activation(term_r[c][:, m], term_r[c][:, m], ACT.Copy, scale=cols[:, ONE_MINUS_LOW, c:c + 1])
 
         x_t = {}
+        x_t_first = []
         x_acc = {}
 
-        def x_t_tiles(b):
+        def open_x_t(b):
             if b == 0:
                 whole = ring.tile([P, CHUNKS, 2, 2, P, 2], BF16, name="x_t", tag="big0", bufs=1, align_bytes=64)
                 for g in range(CHUNKS):
                     x_t[0, g] = whole[:, g]
-                x_t[0] = whole[:].rearrange("m g l u p e -> m (g l) u p e")
+                x_t_first.append(whole[:].rearrange("m g l u p e -> m (g l) u p e"))
             else:
                 for g in range(CHUNKS):
                     x_t[1, g] = keep.tile([P, 2, 2, P, 2], BF16, name="x_t1_%d" % g)[:]
 
-        def sum_terms(c, m0, m1):
-            b, cl = divmod(c, 4)
-            if (b, 0) not in x_t:
-                x_t_tiles(b)
-            blocks = (m1 - m0) // P
-            total = bank("xs")
-            for l in range(blocks):
-                m = slice(m0 + l * P, m0 + (l + 1) * P)
-                for term in range(3):
-                    nc.tensor.matmul(
-                        total[:, l * P:(l + 1) * P], lhsT=(term_e, diff, term_r)[term][c][:, m], rhs=ident[:],
-                        start=(term == 0), stop=(term == 2), is_transpose=True,
-                    )
-            x_acc[c, m0] = total
+        def by_word(acc):
+            return acc.rearrange("m (l q u e) -> m l u q e", u=2, e=2, q=QUAD)
 
-        def round_x(c, m0, m1):
-            b, cl = divmod(c, 4)
-            rounded = x_acc[c, m0][:].rearrange("m (l q u e) -> m l u q e", u=2, e=2, q=32)
-            if b == 0:
-                nc.scalar.copy(x_t[0][:, m0 // P:m1 // P, :, 32 * cl:32 * (cl + 1), :], rounded)
-            else:
-                for i in range(2):
-                    nc.scalar.copy(x_t[1, m0 // CHUNK + i][:, :, :, 32 * cl:32 * (cl + 1), :], rounded[:, 2 * i:2 * i + 2])
+        def own_part(c):
+            return slice(QUAD * (c % PER_PASS), QUAD * (c % PER_PASS + 1))
 
-        def last_diff(c, g):
-            m = slice(g * CHUNK, (g + 1) * CHUNK)
+        def sum_terms(c):
+            if c % PER_PASS == 0:
+                open_x_t(c // PER_PASS)
+            for i, half in enumerate(halves):
+                x_acc[c, i] = bank("xs")
+                for blk in range(4):
+                    m = slice(half.start + blk * P, half.start + (blk + 1) * P)
+                    add_turned(x_acc[c, i][:, blk * P:(blk + 1) * P], [term_e[c][:, m], diff[c][:, m], term_r[c][:, m]])
+
+        def round_x(c):
+            for i in range(2):
+                summed = by_word(x_acc[c, i][:])
+                if c < PER_PASS:
+                    nc.scalar.copy(x_t_first[0][:, 4 * i:4 * i + 4, :, own_part(c), :], summed)
+                else:
+                    for g in range(2):
+                        nc.scalar.copy(x_t[1, 2 * i + g][:, :, :, own_part(c), :], summed[:, 2 * g:2 * g + 2])
+
+        chunks = [slice(g * CHUNK, (g + 1) * CHUNK) for g in range(CHUNKS)]
+
+        def last_diff(g):
+            m = chunks[g]
             nc.vector.tensor_tensor(
-                last_d[:, m], pages[c][:].indirect(idx_after[:, g * CHUNK // 16:(g + 1) * CHUNK // 16]), before[c][:, m],
-                ALU.subtract,
+                last_d[:, m], pages[LAST][:].indirect(entries(idx_after, m)), before[LAST][:, m], ALU.subtract
             )
 
-        def last_term(c, g):
-            m = slice(g * CHUNK, (g + 1) * CHUNK)
-            nc.vector.tensor_scalar(last_r[:, m], last_d[:, m], 0.0, cols[:, 4, c:c + 1], ALU.min, ALU.mult)
-
-        def last_sum(c, g):
-            total = bank("xs")
-            for l in range(2):
-                m = slice(g * CHUNK + l * P, g * CHUNK + (l + 1) * P)
-                for term in range(3):
-                    nc.tensor.matmul(
-                        total[:, l * P:(l + 1) * P], lhsT=(term_e[c], last_d, last_r)[term][:, m], rhs=ident[:],
-                        start=(term == 0), stop=(term == 2), is_transpose=True,
-                    )
-            nc.scalar.copy(
-                x_t[1, g][:, :, :, 96:128, :],
-                total[:, 0:CHUNK].rearrange("m (l q u e) -> m l u q e", u=2, e=2, q=32),
+        def last_relu_term(g):
+            m = chunks[g]
+            nc.vector.tensor_scalar(
+                last_r[:, m], last_d[:, m], 0.0, cols[:, LOW_MINUS_ONE, LAST:LAST + 1], ALU.min, ALU.mult
             )
+
+        def last_sum_on_tensor(g):
+            acc = bank("xs")
+            for blk in range(2):
+                m = slice(g * CHUNK + blk * P, g * CHUNK + (blk + 1) * P)
+                add_turned(acc[:, blk * P:(blk + 1) * P], [term_e[LAST][:, m], last_d[:, m], last_r[:, m]])
+            nc.scalar.copy(x_t[1, g][:, :, :, own_part(LAST), :], by_word(acc[:, 0:CHUNK]))
+
+        last_x = keep.tile([P, (CHUNKS - TENSOR_CHUNKS) * CHUNK], BF16, name="last_x")
+
+        def last_linear_on_vector(g):
+            m = chunks[g]
+            nc.vector.tensor_tensor(last_d[:, m], last_d[:, m], term_e[LAST][:, m], ALU.add)
+
+        def last_sum_on_vector(g):
+            m = chunks[g]
+            x = last_x[:, chunks[g - TENSOR_CHUNKS]]
+            nc.vector.tensor_tensor(x, last_d[:, m], last_r[:, m], ALU.add)
+            turned = psum.tile([P, CHUNK], BF16, name="xs_bf", tag="xs")
+            for blk in range(2):
+                nc.tensor.transpose(turned[:, blk * P:(blk + 1) * P], x[:, blk * P:(blk + 1) * P], ident_bf[:])
+            nc.scalar.copy(x_t[1, g][:, :, :, own_part(LAST), :], by_word(turned[:]))
 
         x_codes = [keep.tile([P, M], U32, name="x_codes%d" % b, align_bytes=64) for b in range(PASSES)]
         x_sc = [keep.tile([P, M], U8, name="x_sc%d" % b, align_bytes=64) for b in range(PASSES)]
         x_bf = {}
-
         x_turned = {}
 
         def turn_x(b, g):
             words = x_t[b, g].rearrange("m l u p e -> m (l u p e)").bitcast(F32)
-            turned = bank("wd")
+            x_turned[b, g] = bank("wd")
             for i in range(4):
-                nc.tensor.transpose(turned[:, i * P:(i + 1) * P], words[:, i * P:(i + 1) * P], ident[:])
-            x_turned[b, g] = turned
+                nc.tensor.transpose(x_turned[b, g][:, i * P:(i + 1) * P], words[:, i * P:(i + 1) * P], ident[:])
 
-        def weave_x(b, g, copy):
-            x_bf[b, g] = ring.tile([P, CHUNK * 4], BF16, name="x_bf", tag="x_bf", bufs=4, align_bytes=64)
-            copy(
+        def weave_x(b, g):
+            x_bf[b, g] = ring.tile([P, CHUNK * 4], BF16, name="x_bf", tag="x_bf", bufs=CHUNKS, align_bytes=64)
+            nc.scalar.copy(
                 x_bf[b, g][:].bitcast(F32).rearrange("p (l m u) -> p l m u", l=2, u=2),
                 x_turned[b, g][:].rearrange("p (l u m) -> p l m u", l=2, u=2),
             )
 
         def quantise_x(b, g):
-            m = slice(g * CHUNK, (g + 1) * CHUNK)
-            nc.vector.quantize_mx(x_codes[b][:, m].bitcast(FP8X4), x_sc[b][:, m], x_bf[b, g][:])
+            nc.vector.quantize_mx(x_codes[b][:, chunks[g]].bitcast(FP8X4), x_sc[b][:, chunks[g]], x_bf[b, g][:])
 
         y_codes = keep.tile([P, M], U32, name="y_codes", align_bytes=64)
         y_sc = keep.tile([P, M], U8, name="y_sc", align_bytes=64)
         y_view = out_0.rearrange("(p t) m -> p t m", t=4)
         y_words = out_1[0].rearrange("p m t -> p (m t)").bitcast(I32)
+        y_acc = {}
         y_sb = {}
         y_bf = {}
 
-        y_acc = {}
-
         def y_pass(g, b):
-            m = slice(g * CHUNK, (g + 1) * CHUNK)
-            for h in range(2):
+            m = chunks[g]
+            for pair in range(2):
                 if b == 0:
-                    y_acc[g, h] = bank(("a", "u")[h])
+                    y_acc[g, pair] = bank(("a", "u")[pair])
                 for i in range(2):
                     nc.tensor.matmul_mx(
-                        y_acc[g, h][:, i * CHUNK:(i + 1) * CHUNK],
-                        lhsT=w2_codes[:, b, 2 * h + i, :].bitcast(FP4X4), lhsT_scale=w2_sc[:, b, 2 * h + i, :],
+                        y_acc[g, pair][:, i * CHUNK:(i + 1) * CHUNK],
+                        lhsT=w2_codes[:, b, 2 * pair + i, :].bitcast(FP4X4), lhsT_scale=w2_sc[:, b, 2 * pair + i, :],
                         rhs=x_codes[b][:, m].bitcast(FP8X4), rhs_scale=x_sc[b][:, m],
                         start=(b == 0 and i == 0), stop=(b == PASSES - 1 and i == 1),
                     )
 
         def store_y(g):
-            m = slice(g * CHUNK, (g + 1) * CHUNK)
-            y_sb[g] = ring.tile([P, 4, CHUNK], F32, name="y_sb", tag="before", bufs=4)
-            for h in range(2):
-                nc.scalar.copy(y_sb[g][:, 2 * h:2 * h + 2, :], y_acc[g, h][:].rearrange("p (i m) -> p i m", i=2))
-            nc.sync.dma_start(y_view[:, :, m], y_sb[g][:])
+            y_sb[g] = ring.tile([P, 4, CHUNK], F32, name="y_sb", tag="before", bufs=BEFORE_BUFS)
+            for pair in range(2):
+                copy = nc.vector.tensor_copy if (g, pair) == (CHUNKS - 1, 1) else nc.scalar.copy
+                copy(y_sb[g][:, 2 * pair:2 * pair + 2, :], y_acc[g, pair][:].rearrange("p (i m) -> p i m", i=2))
+            nc.sync.dma_start(y_view[:, :, chunks[g]], y_sb[g][:])
 
         def round_y(g):
             y_bf[g] = ring.tile([P, CHUNK, 4], BF16, name="y_bf", tag="y_bf", align_bytes=64)
             nc.vector.tensor_copy(
-                y_bf[g][:].rearrange("p (g i) t -> p g t i", i=4), y_sb[g][:].rearrange("p t (g i) -> p g t i", i=4)
+                y_bf[g][:].rearrange("p (s i) t -> p s t i", i=4), y_sb[g][:].rearrange("p t (s i) -> p s t i", i=4)
             )
 
         def quantise_y(g):
-            m = slice(g * CHUNK, (g + 1) * CHUNK)
+            m = chunks[g]
             nc.vector.quantize_mx(y_codes[:, m].bitcast(FP8X4), y_sc[:, m], y_bf[g][:].rearrange("p m t -> p (m t)"))
             nc.sync.dma_start(y_words[:, m], y_codes[:, m].bitcast(I32))
 
-        gained_wgs = make_first_h()
+        gained_wgs = first_slice()
         round_w1(1)
         quantise_w1(1)
         first_product(1)
@@ -388,73 +402,70 @@ def tile_list_stay_tension_survey_kernel(
         quantise_w1(2)
         scale_h(1)
         first_product(2)
-        last = SLICES - 1
-        halves = [(h * BANK, (h + 1) * BANK) for h in range(2)]
         for c in range(SLICES):
-            if 4 <= c + 3 < SLICES:
+            if PAGE_BUFS <= c + 3 < SLICES:
                 load_page(c + 3)
-            put(c, 1, gained_wgs if c == 0 else wgs_sb)
+            put(c, gained_wgs if c == 0 else wgs_sb)
             if c + 2 < SLICES:
                 gather_before(c + 2)
             if c == 1:
-                nc.vector.tensor_copy(w2_sc[:], w2_sc_raw[:].rearrange("p a (q t) -> p a t q", t=4))
-            if c < last:
-                gather_diff(c, 0, M)
+                deal_w2_scales()
+            if c < LAST:
+                gather_diff(c)
             if c >= 1:
-                for m0, m1 in (halves if c == last else [(0, M)]):
-                    diff_terms(c - 1, m0, m1)
-                for m0, m1 in halves:
-                    sum_terms(c - 1, m0, m1)
+                relu_term(c - 1, halves if c == LAST else [slice(0, M)])
+                sum_terms(c - 1)
             if c + 2 < SLICES:
                 read_product(c + 2)
                 add_tanh(c + 2)
-            if c in (5, 6):
-                for g in (2 * c - 10, 2 * c - 9):
-                    weave_x(0, g, nc.scalar.copy)
+            if c - PER_PASS in (1, 2):
+                for g in (2 * (c - PER_PASS - 1), 2 * (c - PER_PASS - 1) + 1):
+                    weave_x(0, g)
                     quantise_x(0, g)
             scale_before(c)
             if c + 3 < SLICES:
                 round_w1(c + 3)
                 quantise_w1(c + 3)
             if c >= 1:
-                for m0, m1 in halves:
-                    round_x(c - 1, m0, m1)
+                round_x(c - 1)
             if c + 2 < SLICES:
                 scale_h(c + 2)
             if c + 3 < SLICES:
                 first_product(c + 3)
-            if c in (4, 5):
-                for g in (2 * c - 8, 2 * c - 7):
+            if c - PER_PASS in (0, 1):
+                for g in (2 * (c - PER_PASS), 2 * (c - PER_PASS) + 1):
                     turn_x(0, g)
 
-        last_r = ring.tile([P, M], F32, name="last_r", tag="h_rows", bufs=3)
+        last_r = ring.tile([P, M], F32, name="last_r", tag="h_rows", bufs=H_BUFS)
         last_d = ring.tile([P, M], F32, name="last_d", tag="tanh_t")
         y_pass(0, 0)
         y_pass(1, 0)
-        for step in range(CHUNKS + 5):
-            if step < CHUNKS:
-                last_diff(last, step)
-            g = step - 1
-            if 0 <= g < CHUNKS:
-                last_term(last, g)
-                last_sum(last, g)
-            g = step - 2
-            if 0 <= g < CHUNKS:
-                turn_x(1, g)
-                weave_x(1, g, nc.scalar.copy if g < 2 else nc.vector.tensor_copy)
-            g = step - 3
-            if 0 <= g < CHUNKS:
-                quantise_x(1, g)
-                y_pass(g, 1)
-                store_y(g)
-                if g + 2 < CHUNKS:
-                    y_pass(g + 2, 0)
-            g = step - 4
-            if 0 <= g < CHUNKS:
-                round_y(g)
-            g = step - 5
-            if 0 <= g < CHUNKS:
-                quantise_y(g)
+
+        def add_terms(g):
+            last_relu_term(g)
+            if g < TENSOR_CHUNKS:
+                last_sum_on_tensor(g)
+            else:
+                last_linear_on_vector(g)
+
+        def lay_out_x(g):
+            if g >= TENSOR_CHUNKS:
+                last_sum_on_vector(g)
+            turn_x(1, g)
+            weave_x(1, g)
+
+        def finish_product(g):
+            quantise_x(1, g)
+            y_pass(g, 1)
+            store_y(g)
+            if g + 2 < CHUNKS:
+                y_pass(g + 2, 0)
+
+        stages = [last_diff, add_terms, lay_out_x, finish_product, round_y, quantise_y]
+        for step in range(CHUNKS + len(stages) - 1):
+            for lag, stage in enumerate(stages):
+                if 0 <= step - lag < CHUNKS:
+                    stage(step - lag)
 
         for q in range(4):
-            nc.sync.dma_start(out_2[0, 4 * q:4 * q + 4, :].bitcast(I32), y_sc[32 * q:32 * q + 4, :].bitcast(I32))
+            nc.sync.dma_start(out_2[0, 4 * q:4 * q + 4, :].bitcast(I32), y_sc[QUAD * q:QUAD * q + 4, :].bitcast(I32))

from contextlib import ExitStack

import concourse.mybir as mybir
from concourse.masks import make_identity

K, H, N, T, S, T2, M = 1024, 1024, 512, 4096, 1024, 2048, 1024
FLOPS = 2 * K * H * S + 2 * H * N * M

F32 = mybir.dt.float32
BF16 = mybir.dt.bfloat16
I32 = mybir.dt.int32
U32 = mybir.dt.uint32
U16 = mybir.dt.uint16
U8 = mybir.dt.uint8
FP8X4 = mybir.dt.float8_e4m3fn_x4
FP4X4 = mybir.dt.float4_e2m1fn_x4
ALU = mybir.AluOpType
ACT = mybir.ActivationFunctionType

P = 128
BANK = 512
STRIPE = 16
SLICES = H // P
PASSES = 2
PER_PASS = SLICES // PASSES
QUAD = P // PER_PASS
LAST = SLICES - 1
CHUNK = 256
CHUNKS = M // CHUNK
TENSOR_CHUNKS = 2
GAIN, LOW, ONE_PLUS_LOW, ONE_MINUS_LOW, LOW_MINUS_ONE = range(5)
PAGE_BUFS, BEFORE_BUFS, H_BUFS, W1_BUFS = 4, 4, 3, 3


def tile_list_stay_tension_survey_kernel(
    tc, tab_words, tab_scales, offs, offs2, offs3, offs4, w1, gain, wgs, page0, low, w2_words, w2_scales,
    out_0, out_1, out_2,
):
    nc = tc.nc
    with ExitStack() as ctx:
        keep = ctx.enter_context(tc.tile_pool(name="keep", bufs=1))
        ring = ctx.enter_context(tc.tile_pool(name="ring", bufs=2))
        psum = ctx.enter_context(tc.psum_pool(name="psum", bufs=2))

        def bank(tag):
            return psum.tile([P, BANK], F32, name=tag, tag=tag)

        idx_tab = keep.tile([P, S // STRIPE], U16, name="idx_tab")
        idx_put = keep.tile([P, S // STRIPE], U16, name="idx_put")
        idx_after = keep.tile([P, M // STRIPE], U16, name="idx_after")
        idx_before = keep.tile([P, M // STRIPE], U16, name="idx_before")

        tab_sc = keep.tile([P, T], U8, name="tab_sc", align_bytes=64)
        w2_sc_raw = keep.tile([P, PASSES, N], U8, name="w2_sc_raw")
        rows = keep.tile([P, P], F32, name="rows")
        nc.vector.memset(tab_sc[:].bitcast(I32), 0)
        nc.vector.memset(w2_sc_raw[:].rearrange("p a n -> p (a n)").bitcast(I32), 0)
        nc.vector.memset(rows[:], 0.0)
        ident = keep.tile([P, P], F32, name="ident")
        make_identity(nc, ident[:])
        ident_bf = keep.tile([P, P], BF16, name="ident_bf")
        make_identity(nc, ident_bf[:])

        pages = {}
        w1_raw = {}

        def load_page(c):
            pages[c] = ring.tile([P, T2], F32, name="page", tag="page", bufs=PAGE_BUFS)
            nc.sync.dma_start(pages[c][:], page0[c * P:(c + 1) * P, :])

        def load_w1(c0, c1):
            raw = keep.tile([P, PASSES, 4, (c1 - c0) * P], F32, name="w1_raw%d" % c0)
            view = w1.rearrange("(a p j) r -> a p j r", p=P, j=4)
            for a in range(PASSES):
                nc.sync.dma_start(raw[:, a], view[a, :, :, c0 * P:c1 * P])
            for c in range(c0, c1):
                w1_raw[c] = raw[:, :, :, (c - c0) * P:(c - c0 + 1) * P]

        tab = [ring.tile([P, T], I32, name="tab", tag="big%d" % a, bufs=1, align_bytes=64) for a in range(PASSES)]

        def load_tab(a):
            nc.sync.dma_start(tab[a][:], tab_words[a].rearrange("p t i -> p (t i)").bitcast(I32))

        nc.sync.dma_start(idx_tab[:], offs)
        load_tab(0)
        load_w1(0, 1)
        w2_raw = keep.tile([P, PASSES, 2 * N], U8, name="w2_raw")
        nc.sync.dma_start(w2_raw[:].bitcast(I32), w2_words.rearrange("a p n -> p a n").bitcast(I32))
        load_tab(1)
        nc.sync.dma_start(idx_before[:], offs4)
        load_page(0)
        wgs_sb = keep.tile([P, S], F32, name="wgs_sb")
        nc.sync.dma_start(wgs_sb[:], wgs)
        nc.sync.dma_start(idx_put[:], offs2)
        load_w1(1, 2)
        nc.sync.dma_start(idx_after[:], offs3)
        load_page(1)
        load_page(2)
        load_w1(2, PER_PASS)
        for q in range(4):
            nc.sync.dma_start(
                w2_sc_raw[QUAD * q:QUAD * q + 4].bitcast(I32),
                w2_scales[:, 4 * q:4 * q + 4, :].rearrange("a r n -> r a n").bitcast(I32),
            )
        load_page(3)
        load_w1(PER_PASS, SLICES)

        for q in range(4):
            nc.gpsimd.dma_start(
                tab_sc[QUAD * q:QUAD * q + 4 * PASSES, :].bitcast(I32), tab_scales[:, 4 * q:4 * q + 4, :].bitcast(I32)
            )
        nc.gpsimd.dma_start(rows[0:SLICES, :], gain.rearrange("(c p) -> c p", p=P))
        nc.gpsimd.dma_start(rows[SLICES:2 * SLICES, :], low.rearrange("(c p) -> c p", p=P))

        w2_codes = keep.tile([P, PASSES, 4, 2 * P], U8, name="w2_codes", align_bytes=64)
        w2_sc = keep.tile([P, PASSES, 4, P], U8, name="w2_sc", align_bytes=64)
        nc.vector.tensor_copy(
            w2_codes[:].rearrange("p a t (q b) -> p a t q b", b=2),
            w2_raw[:].rearrange("p a (q t b) -> p a t q b", t=4, b=2),
        )

        def deal_w2_scales():
            nc.vector.tensor_copy(w2_sc[:], w2_sc_raw[:].rearrange("p a (q t) -> p a t q", t=4))

        before = {}

        def gather_before(c):
            if c == 0:
                pair = ring.tile([P, 2, M], F32, name="before_pair", tag="big1", bufs=1, align_bytes=64)
                before[0], before[1] = pair[:, 0, :], pair[:, 1, :]
            elif c >= 2:
                before[c] = ring.tile([P, M], F32, name="before", tag="before", bufs=BEFORE_BUFS)
            nc.vector.tensor_copy(before[c][:], pages[c][:].indirect(idx_before[:]))

        w1_bf = {}
        w1_q = {}

        def round_w1(c):
            w1_bf[c] = ring.tile([P, PASSES, P, 4], BF16, name="w1_bf", tag="w1_bf", align_bytes=64)
            nc.scalar.copy(
                w1_bf[c][:].rearrange("p a (g i) j -> p a g j i", i=4),
                w1_raw[c].rearrange("p a j (g i) -> p a g j i", i=4),
            )

        def quantise_w1(c):
            codes = ring.tile([P, PASSES * P], U32, name="w1_codes", tag="w1_codes", bufs=W1_BUFS, align_bytes=64)
            scales = ring.tile([P, PASSES * P], U8, name="w1_scales", tag="w1_scales", bufs=W1_BUFS, align_bytes=64)
            nc.vector.quantize_mx(codes[:].bitcast(FP8X4), scales[:], w1_bf[c][:].rearrange("p a r j -> p (a r j)"))
            w1_q[c] = (codes, scales)

        round_w1(0)
        quantise_w1(0)
        v_sc = keep.tile([P, S], U8, name="v_sc", align_bytes=64)
        nc.vector.tensor_copy(v_sc[:], tab_sc[:].indirect(idx_tab[:]))
        v_codes = [keep.tile([P, S], U32, name="v_codes%d" % a, align_bytes=64) for a in range(PASSES)]
        nc.vector.tensor_copy(v_codes[0][:], tab[0][:].bitcast(U32).indirect(idx_tab[:]))
        cols_ps = bank("wd")
        nc.tensor.transpose(cols_ps[:, 0:P], rows[:], ident[:])
        cols = keep.tile([P, 5, SLICES], F32, name="cols")
        nc.vector.tensor_copy(cols[:, GAIN:LOW + 1, :], cols_ps[:, 0:2 * SLICES].rearrange("p (k c) -> p k c", k=2))
        nc.vector.tensor_scalar(cols[:, ONE_PLUS_LOW, :], cols[:, LOW, :], 1.0, 1.0, ALU.mult, ALU.add)
        nc.vector.tensor_scalar(cols[:, ONE_MINUS_LOW, :], cols[:, LOW, :], -1.0, 1.0, ALU.mult, ALU.add)
        nc.vector.tensor_scalar(cols[:, LOW_MINUS_ONE, :], cols[:, LOW, :], 1.0, -1.0, ALU.mult, ALU.add)

        halves = [slice(i * BANK, (i + 1) * BANK) for i in range(2)]

        def entries(tile, span):
            return tile[:, span.start // STRIPE:span.stop // STRIPE]

        for half in halves:
            nc.vector.tensor_copy(v_codes[1][:, half], tab[1][:].bitcast(U32).indirect(entries(idx_tab, half)))

        gather_before(0)

        h_rows = {}
        a_acc = {}
        a_t = {}
        tanh_t = {}
        h_acc = {}

        def first_product(c):
            codes, scales = w1_q[c]
            for i, half in enumerate(halves):
                a_acc[c, i] = bank("a")
                for blk in range(4):
                    j = slice(half.start + blk * P, half.start + (blk + 1) * P)
                    for a in range(PASSES):
                        nc.tensor.matmul_mx(
                            a_acc[c, i][:, blk * P:(blk + 1) * P],
                            lhsT=v_codes[a][:, j].bitcast(FP8X4), lhsT_scale=v_sc[4 * a:P, j],
                            rhs=codes[:, a * P:(a + 1) * P].bitcast(FP8X4), rhs_scale=scales[:, a * P:(a + 1) * P],
                            start=(a == 0), stop=(a == PASSES - 1),
                        )

        def read_product(c):
            a_t[c] = ring.tile([P, S], F32, name="a_t", tag="shared%d" % (c % 2), bufs=1)
            tanh_t[c] = ring.tile([P, S], F32, name="tanh_t", tag="tanh_t")
            for i, half in enumerate(halves):
                nc.scalar.activation(tanh_t[c][:, half], a_acc[c, i][:], ACT.Tanh)
                nc.scalar.copy(a_t[c][:, half], a_acc[c, i][:])

        def add_turned(out, terms):
            for i, term in enumerate(terms):
                nc.tensor.matmul(
                    out, lhsT=term, rhs=ident[:], start=(i == 0), stop=(i == len(terms) - 1), is_transpose=True
                )

        def add_tanh(c):
            for i, half in enumerate(halves):
                h_acc[c, i] = bank("u")
                for blk in range(4):
                    j = slice(half.start + blk * P, half.start + (blk + 1) * P)
                    add_turned(h_acc[c, i][:, blk * P:(blk + 1) * P], [tanh_t[c][:, j], a_t[c][:, j]])

        def scale_h(c):
            h_rows[c] = ring.tile([P, S], F32, name="h_rows", tag="h_rows", bufs=H_BUFS)
            for i, half in enumerate(halves):
                nc.scalar.activation(h_rows[c][:, half], h_acc[c, i][:], ACT.Copy, scale=cols[:, GAIN, c:c + 1])

        def first_slice():
            codes, scales = w1_q[0]
            h_rows[0] = ring.tile([P, S], F32, name="h_rows", tag="h_rows", bufs=H_BUFS)
            tanh_r = ring.tile([P, S], F32, name="tanh_r", tag="tanh_t")
            gained = ring.tile([P, S], F32, name="gained", tag="term_r")
            nc.scalar.activation(gained[:], wgs_sb[:], ACT.Copy, scale=cols[:, GAIN, 0:1])
            for half in halves:
                acc = bank("a")
                for a in range(PASSES):
                    nc.tensor.matmul_mx(
                        acc[:],
                        lhsT=codes[:, a * P:(a + 1) * P].bitcast(FP8X4), lhsT_scale=scales[:, a * P:(a + 1) * P],
                        rhs=v_codes[a][:, half].bitcast(FP8X4), rhs_scale=v_sc[4 * a:P, half],
                        start=(a == 0), stop=(a == PASSES - 1),
                    )
                nc.scalar.activation(tanh_r[:, half], acc[:], ACT.Tanh)
                nc.vector.tensor_tensor(h_rows[0][:, half], acc[:], tanh_r[:, half], ALU.add)
            return gained

        def put(c, weight):
            nc.vector.tensor_tensor(pages[c][:].indirect(idx_put[:]), h_rows[c][:], weight[:], ALU.mult)

        diff = {}
        term_e = {}
        term_r = {}

        def gather_diff(c):
            diff[c] = ring.tile([P, M], F32, name="diff", tag="shared%d" % ((c + 1) % 2), bufs=1)
            nc.vector.tensor_tensor(diff[c][:], pages[c][:].indirect(idx_after[:]), before[c][:], ALU.subtract)

        def scale_before(c):
            term_e[c] = ring.tile([P, M], F32, name="term_e", tag="term_e")
            nc.scalar.activation(term_e[c][:], before[c][:], ACT.Copy, scale=cols[:, ONE_PLUS_LOW, c:c + 1])

        def relu_term(c, spans):
            term_r[c] = ring.tile([P, M], F32, name="term_r", tag="term_r")
            for m in spans:
                nc.scalar.activation(term_r[c][:, m], diff[c][:, m], ACT.Relu, scale=-1.0)
                nc.scalar.activation(term_r[c][:, m], term_r[c][:, m], ACT.Copy, scale=cols[:, ONE_MINUS_LOW, c:c + 1])

        x_t = {}
        x_t_first = []
        x_acc = {}

        def open_x_t(b):
            if b == 0:
                whole = ring.tile([P, CHUNKS, 2, 2, P, 2], BF16, name="x_t", tag="big0", bufs=1, align_bytes=64)
                for g in range(CHUNKS):
                    x_t[0, g] = whole[:, g]
                x_t_first.append(whole[:].rearrange("m g l u p e -> m (g l) u p e"))
            else:
                for g in range(CHUNKS):
                    x_t[1, g] = keep.tile([P, 2, 2, P, 2], BF16, name="x_t1_%d" % g)[:]

        def by_word(acc):
            return acc.rearrange("m (l q u e) -> m l u q e", u=2, e=2, q=QUAD)

        def own_part(c):
            return slice(QUAD * (c % PER_PASS), QUAD * (c % PER_PASS + 1))

        def sum_terms(c):
            if c % PER_PASS == 0:
                open_x_t(c // PER_PASS)
            for i, half in enumerate(halves):
                x_acc[c, i] = bank("xs")
                for blk in range(4):
                    m = slice(half.start + blk * P, half.start + (blk + 1) * P)
                    add_turned(x_acc[c, i][:, blk * P:(blk + 1) * P], [term_e[c][:, m], diff[c][:, m], term_r[c][:, m]])

        def round_x(c):
            for i in range(2):
                summed = by_word(x_acc[c, i][:])
                if c < PER_PASS:
                    nc.scalar.copy(x_t_first[0][:, 4 * i:4 * i + 4, :, own_part(c), :], summed)
                else:
                    for g in range(2):
                        nc.scalar.copy(x_t[1, 2 * i + g][:, :, :, own_part(c), :], summed[:, 2 * g:2 * g + 2])

        chunks = [slice(g * CHUNK, (g + 1) * CHUNK) for g in range(CHUNKS)]

        def last_diff(g):
            m = chunks[g]
            nc.vector.tensor_tensor(
                last_d[:, m], pages[LAST][:].indirect(entries(idx_after, m)), before[LAST][:, m], ALU.subtract
            )

        def last_relu_term(g):
            m = chunks[g]
            nc.vector.tensor_scalar(
                last_r[:, m], last_d[:, m], 0.0, cols[:, LOW_MINUS_ONE, LAST:LAST + 1], ALU.min, ALU.mult
            )

        def last_sum_on_tensor(g):
            acc = bank("xs")
            for blk in range(2):
                m = slice(g * CHUNK + blk * P, g * CHUNK + (blk + 1) * P)
                add_turned(acc[:, blk * P:(blk + 1) * P], [term_e[LAST][:, m], last_d[:, m], last_r[:, m]])
            nc.scalar.copy(x_t[1, g][:, :, :, own_part(LAST), :], by_word(acc[:, 0:CHUNK]))

        last_x = keep.tile([P, (CHUNKS - TENSOR_CHUNKS) * CHUNK], BF16, name="last_x")

        def last_linear_on_vector(g):
            m = chunks[g]
            nc.vector.tensor_tensor(last_d[:, m], last_d[:, m], term_e[LAST][:, m], ALU.add)

        def last_sum_on_vector(g):
            m = chunks[g]
            x = last_x[:, chunks[g - TENSOR_CHUNKS]]
            nc.vector.tensor_tensor(x, last_d[:, m], last_r[:, m], ALU.add)
            turned = psum.tile([P, CHUNK], BF16, name="xs_bf", tag="xs")
            for blk in range(2):
                nc.tensor.transpose(turned[:, blk * P:(blk + 1) * P], x[:, blk * P:(blk + 1) * P], ident_bf[:])
            nc.scalar.copy(x_t[1, g][:, :, :, own_part(LAST), :], by_word(turned[:]))

        x_codes = [keep.tile([P, M], U32, name="x_codes%d" % b, align_bytes=64) for b in range(PASSES)]
        x_sc = [keep.tile([P, M], U8, name="x_sc%d" % b, align_bytes=64) for b in range(PASSES)]
        x_bf = {}
        x_turned = {}

        def turn_x(b, g):
            words = x_t[b, g].rearrange("m l u p e -> m (l u p e)").bitcast(F32)
            x_turned[b, g] = bank("wd")
            for i in range(4):
                nc.tensor.transpose(x_turned[b, g][:, i * P:(i + 1) * P], words[:, i * P:(i + 1) * P], ident[:])

        def weave_x(b, g):
            x_bf[b, g] = ring.tile([P, CHUNK * 4], BF16, name="x_bf", tag="x_bf", bufs=CHUNKS, align_bytes=64)
            nc.scalar.copy(
                x_bf[b, g][:].bitcast(F32).rearrange("p (l m u) -> p l m u", l=2, u=2),
                x_turned[b, g][:].rearrange("p (l u m) -> p l m u", l=2, u=2),
            )

        def quantise_x(b, g):
            nc.vector.quantize_mx(x_codes[b][:, chunks[g]].bitcast(FP8X4), x_sc[b][:, chunks[g]], x_bf[b, g][:])

        y_codes = keep.tile([P, M], U32, name="y_codes", align_bytes=64)
        y_sc = keep.tile([P, M], U8, name="y_sc", align_bytes=64)
        y_view = out_0.rearrange("(p t) m -> p t m", t=4)
        y_words = out_1[0].rearrange("p m t -> p (m t)").bitcast(I32)
        y_acc = {}
        y_sb = {}
        y_bf = {}

        def y_pass(g, b):
            m = chunks[g]
            for pair in range(2):
                if b == 0:
                    y_acc[g, pair] = bank(("a", "u")[pair])
                for i in range(2):
                    nc.tensor.matmul_mx(
                        y_acc[g, pair][:, i * CHUNK:(i + 1) * CHUNK],
                        lhsT=w2_codes[:, b, 2 * pair + i, :].bitcast(FP4X4), lhsT_scale=w2_sc[:, b, 2 * pair + i, :],
                        rhs=x_codes[b][:, m].bitcast(FP8X4), rhs_scale=x_sc[b][:, m],
                        start=(b == 0 and i == 0), stop=(b == PASSES - 1 and i == 1),
                    )

        def store_y(g):
            y_sb[g] = ring.tile([P, 4, CHUNK], F32, name="y_sb", tag="before", bufs=BEFORE_BUFS)
            for pair in range(2):
                copy = nc.vector.tensor_copy if (g, pair) == (CHUNKS - 1, 1) else nc.scalar.copy
                copy(y_sb[g][:, 2 * pair:2 * pair + 2, :], y_acc[g, pair][:].rearrange("p (i m) -> p i m", i=2))
            nc.sync.dma_start(y_view[:, :, chunks[g]], y_sb[g][:])

        def round_y(g):
            y_bf[g] = ring.tile([P, CHUNK, 4], BF16, name="y_bf", tag="y_bf", align_bytes=64)
            nc.vector.tensor_copy(
                y_bf[g][:].rearrange("p (s i) t -> p s t i", i=4), y_sb[g][:].rearrange("p t (s i) -> p s t i", i=4)
            )

        def quantise_y(g):
            m = chunks[g]
            nc.vector.quantize_mx(y_codes[:, m].bitcast(FP8X4), y_sc[:, m], y_bf[g][:].rearrange("p m t -> p (m t)"))
            nc.sync.dma_start(y_words[:, m], y_codes[:, m].bitcast(I32))

        gained_wgs = first_slice()
        round_w1(1)
        quantise_w1(1)
        first_product(1)
        gather_before(1)
        read_product(1)
        add_tanh(1)
        round_w1(2)
        quantise_w1(2)
        scale_h(1)
        first_product(2)
        for c in range(SLICES):
            if PAGE_BUFS <= c + 3 < SLICES:
                load_page(c + 3)
            put(c, gained_wgs if c == 0 else wgs_sb)
            if c + 2 < SLICES:
                gather_before(c + 2)
            if c == 1:
                deal_w2_scales()
            if c < LAST:
                gather_diff(c)
            if c >= 1:
                relu_term(c - 1, halves if c == LAST else [slice(0, M)])
                sum_terms(c - 1)
            if c + 2 < SLICES:
                read_product(c + 2)
                add_tanh(c + 2)
            if c - PER_PASS in (1, 2):
                for g in (2 * (c - PER_PASS - 1), 2 * (c - PER_PASS - 1) + 1):
                    weave_x(0, g)
                    quantise_x(0, g)
            scale_before(c)
            if c + 3 < SLICES:
                round_w1(c + 3)
                quantise_w1(c + 3)
            if c >= 1:
                round_x(c - 1)
            if c + 2 < SLICES:
                scale_h(c + 2)
            if c + 3 < SLICES:
                first_product(c + 3)
            if c - PER_PASS in (0, 1):
                for g in (2 * (c - PER_PASS), 2 * (c - PER_PASS) + 1):
                    turn_x(0, g)

        last_r = ring.tile([P, M], F32, name="last_r", tag="h_rows", bufs=H_BUFS)
        last_d = ring.tile([P, M], F32, name="last_d", tag="tanh_t")
        y_pass(0, 0)
        y_pass(1, 0)

        def add_terms(g):
            last_relu_term(g)
            if g < TENSOR_CHUNKS:
                last_sum_on_tensor(g)
            else:
                last_linear_on_vector(g)

        def lay_out_x(g):
            if g >= TENSOR_CHUNKS:
                last_sum_on_vector(g)
            turn_x(1, g)
            weave_x(1, g)

        def finish_product(g):
            quantise_x(1, g)
            y_pass(g, 1)
            store_y(g)
            if g + 2 < CHUNKS:
                y_pass(g + 2, 0)

        stages = [last_diff, add_terms, lay_out_x, finish_product, round_y, quantise_y]
        for step in range(CHUNKS + len(stages) - 1):
            for lag, stage in enumerate(stages):
                if 0 <= step - lag < CHUNKS:
                    stage(step - lag)

        for q in range(4):
            nc.sync.dma_start(out_2[0, 4 * q:4 * q + 4, :].bitcast(I32), y_sc[QUAD * q:QUAD * q + 4, :].bitcast(I32))
